import numpy as np, ml_dtypes
CORES = [24,25,26,27,28,29,30,31]
N = 8
BF = ml_dtypes.bfloat16
S, L, RO, WEAR = 4096, 192, 2, 16
def near(rng, home, h):
    q = S // 16
    return np.take_along_axis(np.broadcast_to(home, (N, 8, S)), h * q + rng.integers(0, q, h.shape), 2)
def parts(rng):
    home = np.argsort(rng.random((8, S)), axis=1); hab = np.zeros((8, S), np.int64)
    np.put_along_axis(hab, home, np.broadcast_to(np.arange(S) // (S // 16), (8, S)), 1)
    base = rng.integers(0, 256, (N, 8, 16, 16))
    x = np.clip(np.take_along_axis(base, hab[None, :, None, :], 3) + rng.integers(-60, 61, (N, 8, 16, S)), 0, 255)
    lab = np.argsort(rng.random((N, 8, L)), axis=2); inv = np.argsort(lab, axis=2)
    h = np.broadcast_to((lab % 16)[:, :, None, :], (N, 8, 16, L)).reshape(N, 8, 16 * L)
    m = np.where(rng.random(h.shape) < 0.75, near(rng, home, h), rng.integers(0, S, h.shape)).reshape(N, 8, 16, L)
    h = np.broadcast_to(hab[None, :, None, :], (N, 8, 16, S)).reshape(N, 8, 16 * S)
    nb = np.where(rng.random(h.shape) < 0.6, near(rng, home, h), rng.integers(0, S, h.shape)).reshape(N, 8, 16, S)
    v = hab[None] + 16 * rng.integers(0, L // 16, (N, 8, S))
    own = np.where(rng.random((N, 8, S)) < 0.6, np.take_along_axis(inv, v, 2), rng.integers(0, L, (N, 8, S)))
    return x, nb, m, own, rng.integers(600, 1100, (N, 8))
def pack(x, nb, m, own, th):
    return {"x0": x.reshape(N, 128, S).astype(np.float32).astype(BF), "nb": nb.reshape(N, 128, S).astype(np.int32), "m0": m.reshape(N, 128, L).astype(np.int32),
            "own0": own.reshape(N, 8, S).astype(np.int32), "th": th.reshape(N, 8, 1).astype(np.int32)}
def setup_inputs(rng):
    return pack(*parts(rng))
def setup_inputs_ties(rng):
    x, nb, m, own, th = parts(rng); step = rng.choice(np.array([1, 5, 40]), (N, 8, 1, 1))
    lo = ((256 - 3 * step) * rng.random((N, 8, 1, 1)) * (rng.random((N, 8, 1, 1)) < 0.7)).astype(np.int64)
    x = lo + step * rng.integers(0, 4, x.shape)
    pool = rng.integers(0, S, (N, 8, 3, L)); few = np.take_along_axis(pool, rng.integers(0, 3, m.shape), 2)
    m = np.where(rng.random((N, 8, 1, L)) < 0.7, few, rng.integers(0, S, m.shape))
    th = step[:, :, 0, 0] * rng.integers(14, 19, (N, 8))
    z = int(rng.integers(0, 8)); o = rng.permutation(S); cold, warm = o[:S // 2], o[S // 2:]; h = rng.integers(140, 250, N)
    is_cold = np.zeros(S, bool); is_cold[cold] = True
    x[:, z] = np.where(is_cold, 0, h[:, None, None]) + rng.integers(0, 2, (N, 16, S))
    three = cold[rng.integers(0, S // 2, (N, 3, L))]; m[:, z] = np.take_along_axis(three, rng.integers(0, 3, (N, 16, L)), 1)
    nb[:, z] = warm[rng.integers(0, S - S // 2, (N, 16, S))]; th[:, z] = 16 * h + rng.integers(3, 9, N)
    return pack(x, nb, m, own, th)
def setup_inputs_corners(rng):
    x, nb, m, own, th = parts(rng); K = S // L; ev = (K + 1) // 2; od = K // 2
    q = int(rng.integers(0, N)); p = (q - 1) % N; u = (q - 2) % N; la = np.arange(L); st = np.arange(S)
    turn = [rng.permutation(8) for r in range(N)]; turn[u] = turn[p]
    for r in range(N):
        for i, g in enumerate(turn[r]):
            if i == 0: own[r, g] = int(rng.choice(np.array([0, L - 1, L // 2])))
            if i == 1:
                own[r, g] = rng.permutation(L)[st % L]; m[r, g] = la + L * rng.integers(0, K, (16, L))
            if i == 2: m[r, g] = rng.choice(np.array([0, S - 1, int(rng.integers(0, S))]), (1, L))
            if i == 3: nb[r, g] = st[None, :]
            if i == 4: nb[r, g] = (S - 1) * rng.integers(0, 2, (1, S))
            if i == 5:
                th[r, g] = 0; x[r, g] = rng.integers(0, WEAR + 2, (16, S))
            if i == 6:
                th[r, g] = 4080; own[r, g] = (L - 1) * rng.integers(0, 2, S); m[r, g] = (S - 1) * rng.integers(0, 2, (16, L))
            if i == 7: x[r, g] = int(rng.choice(np.array([0, 7, 255])))
    x[q] = np.where((st // L) % 2 == 0, rng.integers(0, 9, (8, 16, S)), 255 - rng.integers(0, 9, (8, 16, S)))
    x[q] = np.where(st // L == 1, rng.integers(18, 21, (8, 16, S)), x[q])
    nb[q] = rng.integers(0, L, (8, 16, S)) + 2 * L * rng.integers(0, ev, (8, 16, S)); th[q] = 200
    own[q] = np.argsort(rng.random((8, L)), axis=1)[:, st % L]
    m[q] = la + L * (2 * rng.integers(1, od, (8, 16, L)) + 1); m[p] = la + 2 * L * rng.integers(0, ev, (8, 16, L))
    m[u, int(turn[u][0])] = L + la
    return pack(x, nb, m, own, th)
def setup_inputs_ends(rng):
    home = 1 + np.argsort(rng.random((8, S - 3)), axis=1)[:, :L]; homes = np.broadcast_to(home, (N, 8, L))
    c = rng.choice(np.array([0, 1, 8, 15, 16]), (N, 8)); c[0, 0] = 0; c[0, 1] = 16; c[N - 1] = rng.choice(np.array([1, 8, 15]), 8)
    x = 255 * rng.integers(0, 2, (N, 8, 16, S))
    x[..., 0] = 255 * (np.argsort(rng.random((N, 8, 16)), axis=2) < c[:, :, None]); x[..., S - 1] = 255 - x[..., 0]; x[..., S - 2] = 255
    np.put_along_axis(x, np.broadcast_to(home[None, :, None, :], (N, 8, 16, L)), 0, 3)
    nb = (S - 1) * rng.integers(0, 2, (N, 8, 16, S))
    nb = np.where(rng.random(nb.shape) < 0.15, np.take_along_axis(homes, rng.integers(0, L, (N, 8, 16 * S)), 2).reshape(nb.shape), nb)
    side = rng.integers(0, 2, (N, 8, S)); nb[:, :, 15] = (S - 1) * side; nb[:, :, 0] = (S - 1) * (1 - side)
    sig = np.argsort(rng.random((N, 8, L)), axis=2); own = (L - 1) * rng.integers(0, 2, (N, 8, S)); np.put_along_axis(own, homes, sig, 2)
    mix = (S - 1) * rng.integers(0, 2, (N, 8, 16, L)); kind = rng.choice(np.array([0, 1, 2, 3, 3, 3]), (N, 8, 1, L)); kind[N - 2] = 3; kind[N - 1] = rng.integers(0, 2, (8, 1, L))
    place = np.argsort(rng.random((N, 8, 16, L)), axis=2); place[:, :, :, L - 1] = np.array([2, 3, 4, 5, 6, 7, 8, 9, 10, 11, 12, 13, 14, 15, 0, 1])
    two = rng.random((N, 8, 1, L)) < 0.5; two[..., L - 1] = True
    far = np.where((place == 1) | ((place == 2) & two), S - 2, mix)
    keep = np.where((place == 0) | ((place == 3) & two), home[None, :, None, :], far)
    m = np.where(kind == 0, 0, np.where(kind == 1, S - 1, np.where(kind == 2, mix, keep)))
    th = 4080 * rng.integers(0, 2, (N, 8)); th[:, 2] = 0; th[:, 7] = 4080
    i = int(rng.integers(0, 7)); th[N - 1] = 4080; th[N - 1, i] = 0
    g = (i + 1 + int(rng.integers(0, 6))) % 7; a = int(rng.integers(0, L)); nb[N - 1, g, :, home[g, a]] = m[N - 1, g, 0, sig[N - 1, g, a]]
    return pack(x, nb, m, own, th)
def setup_inputs_spread(rng):
    x, nb, m, own, th = parts(rng)
    x = np.minimum(np.exp2(8 * rng.random((N, 8, 1, S))) * rng.random((N, 8, 16, S)) * 1.25, 255.0).astype(np.int64) * (rng.random((N, 8, 1, S)) > 0.0625)
    m = np.minimum((S * rng.random((N, 8, 16, L)) ** (1 + 3 * rng.random((N, 8, 1, L)))).astype(np.int64), S - 1)
    m = np.where(rng.random((N, 8, 1, L)) < 0.5, m, S - 1 - m)
    u = np.minimum((S * rng.random((N, 4, 16, S)) ** 2).astype(np.int64), S - 1); nb[:, 1::2] = u
    own = np.minimum((L * rng.random((N, 8, S)) ** 2).astype(np.int64), L - 1)
    return pack(x, nb, m, own, np.exp2(8 + 3 * rng.random((N, 8))).astype(np.int64))
def check_inputs(d):
    bad = []
    for k, lo, hi in (("x0", 0, 255), ("nb", 0, S - 1), ("m0", 0, S - 1), ("own0", 0, L - 1), ("th", 0, 4080)):
        try:
            v = np.asarray(d[k]).astype(np.float32).astype(np.float64)
            if not np.all((v >= lo) & (v <= hi)): bad.append("range of " + k)
            elif not np.all(v == np.floor(v)): bad.append("whole numbers of " + k)
        except Exception:
            bad.append("form of " + k)
    return bad
def centre(x, m):
    v = np.take_along_axis(x, m.reshape(8, 1, 16 * L), 2).reshape(8, 16, 16, L)
    c = (np.max(v, axis=2) + np.min(v, axis=2)) >> 1
    d = np.add.reduce(np.abs(v - c[:, :, None, :]), axis=1)
    return c, np.argmin(d, axis=1), np.argmax(d, axis=1)
def reference(x0, nb, m0, own0, th):
    X = x0.astype(np.float32).astype(np.int32).reshape(N, 8, 16, S); nbs = nb.astype(np.int64).reshape(N, 8, 16, S)
    M = m0.astype(np.int64).reshape(N, 8, 16, L); O = own0.astype(np.int64).reshape(N, 8, S); T = th.astype(np.int64).reshape(N, 8)
    wins = np.zeros(N, np.int64); lane = np.broadcast_to(np.arange(L), (8, L)); grp = np.broadcast_to(np.arange(8)[:, None], (8, L))
    for t in range(RO):
        res, back = [], []; now = np.zeros(N, np.int64)
        for q in range(N):
            p = (q - 1 - t % (N - 1)) % N
            ci, ki, fi = centre(X[q], M[p]); cr, kr, fr = centre(X[q], M[q])
            s = np.take_along_axis(M[p], ki[:, None, :], 1)[:, 0]
            b = np.take_along_axis(O[q], s, 1)
            low = np.full((8, L), L); np.minimum.at(low, (grp, b), lane)
            fight = np.take_along_axis(low, b, 1) == lane
            n = np.take_along_axis(nbs[q], s[:, None, :], 2)
            v = np.take_along_axis(X[q], n.reshape(8, 1, 16 * L), 2).reshape(8, 16, 16, L)
            ei = np.add.reduce(np.abs(v - ci[:, :, None, :]), axis=1)
            er = np.add.reduce(np.abs(v - np.take_along_axis(cr, b[:, None, :], 2)[:, :, None, :]), axis=1)
            lim = T[q][:, None, None] + (wins[q] & 63)
            won = np.count_nonzero(ei < lim, axis=1) > np.count_nonzero(er < lim, axis=1)
            e = np.where(won[:, None, :], ei, er)
            best = np.take_along_axis(n, np.argmin(e, axis=1)[:, None, :], 1)[:, 0]
            worst = np.take_along_axis(n, np.argmax(e, axis=1)[:, None, :], 1)[:, 0]
            g, a = np.nonzero(fight); w = won[g, a]; bb = b[g, a]; ss = s[g, a]
            res.append((q, g, fr[g, bb], bb, np.where(w, worst[g, a], best[g, a])))
            back.append((p, g, np.where(w, fi[g, a], ki[g, a]), a, np.where(w, best[g, a], worst[g, a])))
            O[q][g, ss] = np.where(w, np.where(bb + 1 == L, 0, bb + 1), bb)
            if t < RO - 1: X[q][g, :, ss] = np.maximum(X[q][g, :, ss] - WEAR, 0)
            now[q] = np.count_nonzero(w)
        for r, g, k, a, z in res + back: M[r][g, k, a] = z
        wins = now
    return {"ym": M.reshape(N, 128, L).astype(np.float32), "yown": O.astype(np.float32)}

@@ -1,0 +1,526 @@
+from concourse.bass import DstId, RemoteDMATransfer
+from concourse.mybir import AluOpType, ActivationFunctionType
+
+OP = AluOpType
+AF = ActivationFunctionType
+F32, BF, I32, U16 = "float32", "bfloat16", "int32", "uint16"
+BIG = float(2 ** 26)
+
+OWN_TILES = {
+    F32: "IC0:192 IC1:192 RC0:384 RC1:384 MR0:192 MR1:192 inA:192 inB:192 inM:192 inC:192 yo:192",
+    BF: "X:4288 ow:4288 FW:4288 ob:256 VI:3072 VR:3072 V2:3072 XI:3072 NI:3072 XR:3072 NR:3072 CZI:3072 CZR:3072 "
+        "CXI:3072 CXR:3072 CXB:3072 DA:3072 DB:3072 m01:1536 m512:1536 mB:1024 meq:2128 EQ:2128 EC:2128 CRc:192 mR:192",
+    I32: "nbw:4096 od:256 mi32:192 thi:1",
+    U16: "oR0:192 oI0:192",
+}
+POOLS = {
+    F32: "pf:1 pp1:1 p15:1 p16:1 cc:128 kk:256 c16:12 IDf:96/96 dA:256/96 B6:6/96 K64:256/96 oneF:96/8 aC:24 TI:256/96 TR:256/96 T2:256/96 "
+         "PI:512/96 PN:512/96 KI:1024/96 FI:1024/96 KR:1024/96 FR:1024/96 KD:256/96 FD:256/96 t16:16/96 kfl:48/96 dk:16/96 dw:16/96 "
+         "ZS:256/96 SXm:256/96 SW:24 sI:192 sR:192 du:12 f2:24 l1:24 l2:24 l3:24 fp:192 mRa:192 ZL:512/96 LX:512/96 thA:16/96 w4:64/96 "
+         "mk:192 s1:64/96 s2:64/96 s5:32/96 ZZ:512/96 ZX:512/96 zr:192 wc:1 wk:1/96 thD:8/8 thf:1/8 mb0:192 mb1:192",
+    BF: "BI1:8 BI2:8 ID:128 dW:192 LT:192 j64:128/1 one1:128/1 oneB:96 HL:384 bf:192 bd:192 bs:192 ZW:192 bx:192 ff:192 ZR:256/96 RX:256/96 "
+        "FM:512/96 CN:512/96 ZK:512/96 KX:512/96 ox:192 oy:192 ov:192 xg:192 wf:192 wg:192 wb:1 V0:192",
+    I32: "pI:1 pJ:1 CiI:192 CiR:192 HL32:384 eD:16/96 fD:16/96 eI:48/96 e63:32/96 kc:48/96 n32:192 s3:64/96 s4:64/96 wi:1/96 wj:1/96 mw:192 mv:192 a32:192",
+    U16: "oI1:192 oR1:192 sL:12 nL:192 bU:192 Lb:12 LS:24 aU:192",
+}
+SCRATCH, SHAPE, PLACE = {}, {}, {}
+for _d, _names in OWN_TILES.items():
+    for _n in _names.split():
+        _n, _w = _n.split(":")
+        _p = 8 if _n == "thi" else 128
+        SCRATCH[_n] = ("sbuf", [_p, int(_w)], _d)
+        SHAPE[_n], PLACE[_n] = (_p, int(_w)), (_n, 0)
+for _d, _names in POOLS.items():
+    _at = 0
+    for _n in _names.split():
+        _n, _w = _n.split(":")
+        _w = (_w + "/128").split("/")
+        SHAPE[_n], PLACE[_n] = (int(_w[1]), int(_w[0])), ("pool_" + _d, _at)
+        _at += -(-int(_w[0]) // 16) * 16
+    SCRATCH["pool_" + _d] = ("sbuf", [128, _at], _d)
+SCRATCH["odr"] = ("dram", [8, 4096], BF)
+PSUM = ["b%d" % _i for _i in range(8)]
+for _n in PSUM:
+    SCRATCH[_n] = ("psum", [128, 512], F32)
+    SHAPE[_n], PLACE[_n] = (128, 512), (_n, 0)
+SEMAPHORES = ["qv", "qa", "qp", "qg"] + ["d%d" % i for i in range(16)] + ["rM", "rA", "rB", "rR", "rC"] + ["l%d" % i for i in range(5)]
+
+
+def rank_program(g, core, T, topo):
+    rank = T.rank_of(core)
+    if rank is None:
+        return
+    n_ranks = len(T.cores)
+    S = T.sem
+    queue = {"v": g.vector, "a": g.scalar, "p": g.tensor, "g": g, "s": g.sync}
+    count = {"v": 0, "a": 0, "p": 0, "g": 0}
+    known = {"v": {}, "a": {}, "p": {}, "g": {}, "s": {}}
+    snap = {}
+    log = {}
+    ndma = [0]
+
+    def R(name, lo=0, hi=None, step=1, p=None):
+        shape = SHAPE[name]
+        hi = shape[1] if hi is None else hi
+        p = shape[0] if p is None else p
+        buf, at = PLACE[name]
+        ap = T[buf][0:p, at + lo:at + hi:step] if step > 1 else T[buf][0:p, at + lo:at + hi]
+        return (ap, [(name, lo, hi)])
+
+    def A(name, lo=0, hi=None, step=1):
+        return R(name, lo, hi, step, 96)
+
+    def IND(win, lo, hi, off, c0, c1):
+        buf, at = PLACE[off]
+        return (T[win][:, lo:hi].indirect(T[buf][:, at + c0:at + c1]), [(win, lo, hi), (off, c0, c1)])
+
+    def learn(q, sem, val):
+        k = known[q]
+        for s2, v2 in snap.get((sem, val), {}).items():
+            k[s2] = max(k.get(s2, 0), v2)
+        k[sem] = max(k.get(sem, 0), val)
+
+    def need(q, reads, writes, skip_own=False):
+        deps = {}
+        for lst, wr in ((reads, False), (writes, True)):
+            for name, lo, hi in lst:
+                for e in log.get(name, ()):
+                    if name in PSUM and e[1] != q:
+                        hit = True
+                    else:
+                        hit = (wr or e[0]) and e[4] < hi and lo < e[5]
+                    if hit and not (skip_own and e[1] == q):
+                        deps[e[2]] = max(deps.get(e[2], 0), e[3])
+        for sem, val in sorted(deps.items(), key=lambda d: -len(snap.get(d, {}))):
+            if known[q].get(sem, 0) < val:
+                queue[q].wait_ge(S[sem], val)
+                learn(q, sem, val)
+
+    def note(q, sem, val, reads, writes):
+        for lst, wr in ((reads, False), (writes, True)):
+            for name, lo, hi in lst:
+                old = log.setdefault(name, [])
+                if wr:
+                    old[:] = [e for e in old if not (lo <= e[4] and e[5] <= hi)]
+                old.append([wr, q, sem, val, lo, hi])
+
+    def spans(refs):
+        return [s for r in refs for s in r[1]]
+
+    def emit(q, call, outs, ins, skip_own=False):
+        rd, wr = spans(ins), spans(outs)
+        need(q, rd, wr, skip_own)
+        count[q] += 1
+        sem = "q" + q
+        call().then_inc(S[sem], 1)
+        snap[(sem, count[q])] = dict(known[q])
+        note(q, sem, count[q], rd, wr)
+
+    def ind_out(o):
+        return (o[0], o[1][:1]), (o[0], o[1][1:])
+
+    def tt(o, a, b, op):
+        emit("v", lambda: g.vector.tensor_tensor(o[0], a[0], b[0], op), [o], [a, b])
+
+    def tt_scatter(o, a, b, op):
+        w, l = ind_out(o)
+        emit("v", lambda: g.vector.tensor_tensor(o[0], a[0], b[0], op), [w], [a, b, l])
+
+    def ts(o, a, s1, op0, s2=None, op1=None):
+        sc1 = s1[0] if isinstance(s1, tuple) else s1
+        ins = [a] + ([s1] if isinstance(s1, tuple) else [])
+        if op1 is None:
+            emit("v", lambda: g.vector.tensor_scalar(o[0], a[0], sc1, None, op0), [o], ins)
+        else:
+            emit("v", lambda: g.vector.tensor_scalar(o[0], a[0], sc1, s2, op0, op1), [o], ins)
+
+    def cp(o, a):
+        emit("v", lambda: g.vector.tensor_copy(o[0], a[0]), [o], [a])
+
+    def cp_scatter(o, a):
+        w, l = ind_out(o)
+        emit("v", lambda: g.vector.tensor_copy(o[0], a[0]), [w], [a, l])
+
+    def ms(o, c):
+        emit("v", lambda: g.vector.memset(o[0], c), [o], [])
+
+    def scan(o, d0, d1, op0, op1):
+        emit("v", lambda: g.vector.tensor_tensor_scan(o[0], d0[0], d1[0], 0.0, op0, op1), [o], [d0, d1])
+
+    def act(o, a, func=AF.Copy, bias=0.0, scale=1.0, acc=None):
+        ins = [a] + ([scale] if isinstance(scale, tuple) else [])
+        sc = scale[0] if isinstance(scale, tuple) else scale
+        if acc is None:
+            emit("a", lambda: g.scalar.activation(o[0], a[0], func, bias=bias, scale=sc), [o], ins)
+        else:
+            emit("a", lambda: g.scalar.activation(o[0], a[0], func, bias=bias, scale=sc, accum_out=acc[0]), [o, acc], ins)
+
+    def mm(o, l, r, start=True, stop=True):
+        emit("p", lambda: g.tensor.matmul(o[0], l[0], r[0], start, stop), [o], [l, r], True)
+
+    def iota(o, pat, base=0, cm=0, flag=True):
+        kw = {"allow_small_or_imprecise_dtypes": True} if flag else {}
+        emit("g", lambda: g.iota(o[0], pat, base, cm, **kw), [o], [])
+
+    def dma(q, pairs):
+        rd, wr = spans([b for a, b in pairs]), spans([a for a, b in pairs])
+        need(q, rd, wr)
+        sem = "d%d" % ndma[0]
+        ndma[0] += 1
+        for a, b in pairs:
+            queue[q].dma_start(a[0], b[0]).then_inc(S[sem], 16)
+        snap[(sem, 16 * len(pairs))] = dict(known[q])
+        note("dma", sem, 16 * len(pairs), rd, wr)
+
+    def ext(t):
+        return (t[:], [])
+
+    nloc = [0]
+    loc_done = []
+
+    def send(src, outs):
+        need("g", [(src, 0, 192)], [])
+        ls = "l%d" % nloc[0]
+        nloc[0] += 1
+        total = 0
+        tr = []
+        for i, (d, land, rs) in enumerate(outs):
+            dst = T.cores[d]
+            rid, pid, _ = topo.addr(dst)
+            es = topo.engines(core, dst)
+            m = len(es) // len(outs)
+            es = es[i * m:(i + 1) * m]
+            total += m
+            tr.append((rid, pid, sum(1 << e for e in es), land, rs))
+        if len(tr) == 1:
+            rid, pid, mask, land, rs = tr[0]
+            g.remote_dma(T[land][:], T[src][:], S[rs], S[ls], pid, rid, mask)
+        else:
+            g.remote_dma_fused([RemoteDMATransfer(dst_ids=[DstId(rid=rid, pnc=pid)], dma_engine_mask=mask, remote_sem=S[rs],
+                                                  src=T[src][:], dst=T[land][:]) for rid, pid, mask, land, rs in tr], local_sem=S[ls])
+        snap[(ls, total)] = dict(known["g"])
+        note("rem", ls, total, [(src, 0, 192)], [])
+        loc_done.append((ls, total))
+
+    def landed(land, sem, val):
+        note("rem", sem, val, [], [(land, 0, 192)])
+
+    up1, up2 = (rank + 1) % n_ranks, (rank + 2) % n_ranks
+    dn1, dn2 = (rank - 1) % n_ranks, (rank - 2) % n_ranks
+    n16 = len(topo.engines(core, T.cores[up1]))
+    H = (0, 1)
+
+    dma("s", [(R("mi32"), ext(T.m0))])
+    dma("s", [(R("X", 0, 4096), ext(T.x0))])
+    dma("a", [(R("od"), ext(T.own0))])
+    dma("a", [(R("thi"), ext(T.th))])
+    dma("s", [(R("nbw"), ext(T.nb))])
+    iota(R("pI"), [[0, 1]], 0, 1, False)
+    iota(R("kk"), [[0, 16], [1, 16]])
+    iota(R("cc"), [[1, 128]])
+    iota(R("c16"), [[16, 12]])
+    iota(R("a32"), [[1, 192]], 0, 0, False)
+    ms(R("m01"), 1.0)
+    ms(R("m01", 0, 1536, 16), 0.0)
+    ms(R("m512"), 0.0)
+    ms(R("m512", 0, 1536, 16), 512.0)
+    for h in H:
+        act(R("CZI", 1536 * h, 1536 * h + 1536), R("m01"), AF.Copy, 0.0, 0.0)
+    cp(R("oR0"), R("mi32"))
+    send("oR0", [(up1, "oI0", "rM")])
+    landed("oI0", "rM", n16)
+    for name, c in (("CZR", 0), ("EQ", 0), ("meq", 1), ("RC0", 0), ("RC1", 0)):
+        iota(R(name), [[0, SHAPE[name][1]]], c)
+    iota(R("FW", 0, 4096), [[0, 4096]], 1)
+    iota(R("FW", 4096, 4288), [[0, 192]], 0)
+    ts(R("pJ"), R("pI"), 15, OP.bitwise_and)
+    cp(R("p15"), R("pJ"))
+    cp(R("pf"), R("pI"))
+    ts(R("pJ"), R("pI"), 4, OP.arith_shift_right)
+    cp(R("p16"), R("pJ"))
+    ts(R("ID"), R("cc"), R("pf"), OP.is_equal)
+    ts(R("BI1"), R("cc", 0, 8), R("p16"), OP.is_equal, 1024.0, OP.mult)
+    ts(R("BI2"), R("cc", 0, 8), R("p16"), OP.is_equal, 2048.0, OP.mult)
+    ms(R("one1"), 1.0)
+    ts(R("K64"), A("kk"), 64.0, OP.mult)
+    cp(R("j64"), R("K64", 0, 128, 1, 1))
+    ms(R("mB"), 0.0)
+    ms(R("mB", 0, 1024, 16), BIG)
+    ms(R("ZS"), 0.0)
+    ts(R("dA"), A("kk"), R("p15", p=96), OP.is_equal)
+    ts(R("B6"), A("cc", 0, 6), R("p16", p=96), OP.is_equal)
+    cp(R("ob"), R("od"))
+    dma("s", [((T.odr[:], [("odr", 0, 4096)]), R("ob"))])
+    dma("s", [((T.ow[r:128:16, 0:4096], [("ow", 0, 4096)]), (T.odr[:], [("odr", 0, 4096)])) for r in range(16)])
+    ts(R("IDf"), A("cc", 0, 96), R("pf", p=96), OP.is_equal)
+    ts(R("dW"), R("kk", 0, 192), R("p15"), OP.is_equal)
+    ts(R("LT"), R("kk", 0, 192), R("p15"), OP.is_ge, 1000.0, OP.mult)
+    ms(R("ZW"), 0.0)
+
+    def late_constants():
+        for name in ("ZK", "ZR", "ZL", "ZZ"):
+            ms(R(name), 0.0)
+        cp(R("aU"), R("a32"))
+        ts(R("pp1"), R("p15"), 1.0, OP.add)
+        ts(R("aC", 0, 12), R("c16"), R("p15"), OP.add, 4096.0, OP.add)
+        ts(R("aC", 12, 24), R("c16"), R("p15"), OP.add, 192.0, OP.add)
+        ms(R("meq", 0, 1936, 176), 0.0)
+        ms(R("meq", 1936, 2128, 16), 0.0)
+        ms(R("X", 4096, 4288), 0.0)
+        ms(R("ow", 4096, 4288), 0.0)
+        ms(R("oneB"), 1.0)
+        ms(R("oneF"), 1.0)
+        cp(R("mb0"), R("mi32"))
+        cp(R("thf"), R("thi"))
+        ts(R("thD"), R("IDf", 0, 8, 1, 8), R("thf"), OP.mult)
+        mm(R("b6", 0, 8, 1, 96), R("oneF"), R("thD"))
+        for h in H:
+            ts(R("thA", 8 * h, 8 * h + 8), A("b6", 0, 8), 1024.0, OP.mult)
+
+    def half(name, h, step=1):
+        return R(name, 1536 * h, 1536 * h + 1536, step)
+
+    def gather(v, off, h):
+        act(half(v, h), IND("X", 0, 4096, off, 96 * h, 96 * h + 96))
+
+    def group_sum(bank, src, w, h):
+        for k in range(16):
+            mm(A(bank, 128 * h + k, 128 * h + 128, 16), R(src, 1536 * h + k, 1536 * h + 1536, 16), R(w))
+
+    def extremes(v, mx, mn, h):
+        scan(half(mx, h), R("m01"), half(v, h), OP.mult, OP.max)
+        scan(half(mn, h), R("m512"), half(v, h), OP.add, OP.min)
+
+    def centres(mx, mn, s, ci, cz):
+        tt(R(s), R(mx, 15, 3072, 16), R(mn, 15, 3072, 16), OP.add)
+        ts(R(ci), R(s), 0.5, OP.mult, -0.25, OP.add)
+        cp(R(cz, 0, 3072, 16), R(ci))
+
+    def larger(v, first, cx, c0, d, h):
+        tt(half(v, h, 16), first, half(c0, h, 16), OP.max)
+        scan(half(d, h), half(cx, h), half(v, h), OP.min, OP.max)
+
+    def split(m32):
+        ts(R("HL32", 0, 192), R(m32), 6, OP.arith_shift_right)
+        ts(R("HL32", 192, 384), R(m32), 63, OP.bitwise_and)
+        cp(R("HL"), R("HL32"))
+
+    def payload(dst):
+        for i in range(2):
+            for h in H:
+                o = A("b4", 256 * i + 128 * h, 256 * i + 128 * h + 128)
+                mm(o, R("HL", 192 * i + 96 * h, 192 * i + 96 * h + 96), R("ID"), True, False)
+                mm(o, R("one1", 0, 96), R("j64"), False, True)
+        act(R(dst), A("b4"))
+
+    def seg(f, lo, hi):
+        return A(f, lo + 15, hi, 16)
+
+    def play(t):
+        oI, oR, mb = "oI%d" % t, "oR%d" % t, "mb%d" % t
+        IC, RC, MR = "IC%d" % t, "RC%d" % t, "MR%d" % t
+        last = t == 1
+        m96 = R("m01", 0, 256, 1, 96)
+        m96x2 = R("m01", 0, 512, 1, 96)
+        if t == 0:
+            cp(R("mw"), R(oI))
+        for h in H:
+            gather("VI", oI, h)
+        split("mw")
+        for h in H:
+            extremes("VI", "XI", "NI", h)
+        payload("PI")
+        gather("VR", oR, 0)
+        for h in H:
+            group_sum("b2", "VI", "BI1", h)
+        act(R("TI"), A("b2", 0, 256))
+        gather("VR", oR, 1)
+        centres("XI", "NI", "sI", "CiI", "CZI")
+        for h in H:
+            scan(half("CXI", h), R("m01"), half("CZI", h), OP.mult, OP.add)
+            larger("VI", half("VI", h, 16), "CXI", "CZI", "DA", h)
+            group_sum("b0", "DA", "BI2", h)
+        for h in H:
+            group_sum("b2", "VR", "BI1", h)
+        if t == 0:
+            late_constants()
+        extremes("VR", "XR", "NR", 0)
+        u = A("b3", 0, 256)
+        tt(u, A("b0", 0, 256), R("TI"), OP.subtract)
+        tt(R("KI", 0, 256), u, R("PI", 0, 256), OP.add)
+        tt(R("KI", 256, 512), u, R("PI", 256, 512), OP.add)
+        tt(R("KI", 512, 768), R("PI", 0, 256), u, OP.subtract)
+        scan(R("FI", 0, 768), R("mB", 0, 768, 1, 96), R("KI", 0, 768), OP.add, OP.min)
+        cp(R("eI"), seg("FI", 0, 768))
+        ts(R("e63"), R("eI", 0, 32), 63, OP.bitwise_and)
+        ts(R("t16"), R("e63", 0, 16), 64.0, OP.mult)
+        tt(R("ZS", 0, 256, 16), R("t16"), R("e63", 16, 32), OP.add)
+        scan(u, m96, R("ZS"), OP.mult, OP.add)
+        tt(R("SXm"), u, R("dA"), OP.mult)
+        for h in H:
+            mm(R("b7", 6 * h, 6 * h + 6), R("SXm", 128 * h, 128 * h + 128), R("B6"))
+        cp(R("sL"), R("b7", 0, 12))
+        cp(R("nL"), IND("nbw", 0, 4096, "sL", 0, 12))
+        act(R("SW", 0, 12), R("b7", 0, 12))
+        for h in H:
+            gather("V2", "nL", h)
+            act(R("V0", 96 * h, 96 * h + 96), half("V2", h, 16))
+        act(R("TR"), A("b2", 0, 256))
+        cp(R("bf"), IND("ow", 0, 4096, "sL", 0, 12))
+        cp(R("bU"), R("bf"))
+        mm(R("b6", 0, 192), R("ID"), R("bf"), True, False)
+        mm(R("b6", 0, 192), R("ID"), R("LT"), False, True)
+        extremes("VR", "XR", "NR", 1)
+        centres("XR", "NR", "sR", "CiR", "CZR")
+        cp(R("CRc"), R("CiR"))
+        for h in H:
+            act(half("CXB", h), IND("CRc", 0, 192, "bU", 96 * h, 96 * h + 96))
+        cp(R("n32"), R("nL"))
+        split("n32")
+        payload("PN")
+        for h in H:
+            group_sum("b2", "V2", "BI1", h)
+        act(R("T2"), A("b2", 0, 256))
+        for h in H:
+            act(half("CXR", h), IND("CRc", 0, 192, "aU", 96 * h, 96 * h + 96))
+        tt(R("bd"), R("bf"), R("dW"), OP.mult)
+        scan(R("bs"), R("m01", 0, 192), R("bd"), OP.mult, OP.add)
+        cp(R("SW", 12, 24), R("bs", 15, 192, 16))
+        cp(R("ZW", 0, 192, 16), R("bs", 15, 192, 16))
+        cp(R("Lb"), R("SW", 12, 24))
+        for c in range(1, 12):
+            e = 176 * c
+            ts(R("EQ", e - 16 * c, e), R("bf", 0, 16 * c), R("SW", 12 + c, 13 + c), OP.is_equal)
+        scan(R("bx"), R("m01", 0, 192), R("ZW"), OP.mult, OP.add)
+        tt(R("EQ", 1936, 2128), R("b6", 0, 192), R("bx"), OP.is_equal)
+        scan(R("EC"), R("meq"), R("EQ"), OP.mult, OP.add)
+        cp(R("du"), R("EC", 1951, 2128, 16))
+        tt(R("du", 1, 12), R("du", 1, 12), R("EC", 175, 1936, 176), OP.add)
+        ts(R("f2", 0, 12), R("du"), 0.0, OP.is_equal)
+        ts(R("f2", 12, 24), R("du"), 0.0, OP.is_equal)
+        tt(R("l1"), R("SW"), R("aC"), OP.subtract)
+        tt(R("l2"), R("l1"), R("f2"), OP.mult)
+        tt(R("l3"), R("l2"), R("aC"), OP.add)
+        cp(R("LS"), R("l3"))
+        for h in H:
+            larger("V2", R("V0", 96 * h, 96 * h + 96), "CXI", "CZI", "DA", h)
+            group_sum("b0", "DA", "BI2", h)
+        for h in H:
+            larger("VR", half("VR", h, 16), "CXR", "CZR", "DB", h)
+            group_sum("b1", "DB", "BI2", h)
+        act(R("ff"), IND("FW", 0, 4288, "LS", 0, 12))
+        act(R("fp"), R("ff"), AF.Identity, -1.0, R("pp1"))
+        if not last:
+            act(R("xg"), IND("X", 0, 4096, "sL", 0, 12), AF.Relu, -16.0)
+        ur = A("b3", 256, 512)
+        tt(ur, A("b1", 0, 256), R("TR"), OP.subtract)
+        tt(R("KD"), R("K64"), ur, OP.subtract)
+        scan(R("FD"), R("mB", 0, 256, 1, 96), R("KD"), OP.add, OP.min)
+        cp(R("eD"), seg("FD", 0, 256))
+        ts(R("fD"), R("eD"), 6, OP.arith_shift_right, 15, OP.bitwise_and)
+        cp(R("ZR", 0, 256, 16), R("fD"))
+        scan(R("RX"), m96, R("ZR"), OP.mult, OP.add)
+        for h in H:
+            mm(R("b6", 96 * h, 96 * h + 96), R("RX", 128 * h, 128 * h + 128), R("ID", 0, 96, 1, 96))
+        ts(R("mR"), R("b6", 0, 192), R("p15"), OP.is_equal)
+        act(R("mRa"), IND("mR", 0, 192, "Lb", 0, 12))
+        for h in H:
+            larger("V2", R("V0", 96 * h, 96 * h + 96), "CXB", "CXB", "DB", h)
+            group_sum("b1", "DB", "BI2", h)
+        for i, cz in ((0, "CZI"), (1, "CXB")):
+            for h in H:
+                mm(A("b7", 16 + 16 * i + 8 * h, 24 + 16 * i + 8 * h), half(cz, h, 16), R("BI1"))
+        ui = A("b3", 0, 256)
+        tt(ui, A("b0", 0, 256), R("T2"), OP.subtract)
+        hi, lo = R("PN", 0, 256), R("PN", 256, 512)
+        tt(R("KI", 0, 256), ui, hi, OP.add)
+        tt(R("KI", 256, 512), hi, ui, OP.subtract)
+        tt(R("KI", 512, 768), ui, lo, OP.add)
+        tt(R("KI", 768, 1024), lo, ui, OP.subtract)
+        ts(R("kc"), R("eI"), 6, OP.arith_shift_right, 15, OP.bitwise_and)
+        cp(R("kfl"), R("kc"))
+        tt(R("dk"), R("kfl", 32, 48), R("kfl", 0, 16), OP.subtract)
+        scan(R("FI"), A("mB"), R("KI"), OP.add, OP.min)
+        for i in (0, 1):
+            tt(R("ZL", 256 * i, 256 * i + 256, 16), A("b7", 16 + 16 * i, 32 + 16 * i), R("thA"), OP.add)
+        scan(R("LX"), m96x2, R("ZL"), OP.mult, OP.add)
+        tt(R("FM", 0, 256), ui, R("LX", 0, 256), OP.is_lt)
+        tt(ur, A("b1", 0, 256), R("T2"), OP.subtract)
+        tt(R("FM", 256, 512), ur, R("LX", 256, 512), OP.is_lt)
+        scan(R("CN"), m96x2, R("FM"), OP.mult, OP.add)
+        tt(R("w4", 0, 16), seg("CN", 0, 256), seg("CN", 256, 512), OP.is_gt)
+        for i in (1, 2, 3):
+            act(R("w4", 16 * i, 16 * i + 16), R("w4", 0, 16))
+        act(R("ZK", 256, 512, 16), R("w4", 0, 16))
+        tt(R("dw"), R("dk"), R("w4", 0, 16), OP.mult)
+        tt(R("ZK", 0, 256, 16), R("dw"), R("kfl", 0, 16), OP.add)
+        tt(R("KR", 0, 256), hi, ur, OP.subtract)
+        tt(R("KR", 256, 512), ur, hi, OP.add)
+        scan(R("KX"), m96x2, R("ZK"), OP.mult, OP.add)
+        for i in range(4):
+            mm(R("b6", 96 * i, 96 * i + 96), R("KX", 128 * i, 128 * i + 128), R("ID", 0, 96, 1, 96))
+        tt(R("KR", 512, 768), lo, ur, OP.subtract)
+        tt(R("KR", 768, 1024), ur, lo, OP.add)
+        scan(R("FR"), A("mB"), R("KR"), OP.add, OP.min)
+        tt(R("s1"), seg("FI", 0, 1024), seg("FR", 0, 1024), OP.subtract)
+        tt(R("s2"), R("s1"), R("w4"), OP.mult)
+        tt(R("s3"), R("s2"), seg("FR", 0, 1024), OP.add)
+        ts(R("s4"), R("s3"), 63, OP.bitwise_and)
+        ts(R("s5"), R("s4", 0, 32), 64.0, OP.mult, 8192.0, OP.add)
+        tt(R("ZZ", 0, 512, 16), R("s5"), R("s4", 32, 64), OP.add)
+        for i, bank in ((0, "b5"), (1, "b4")):
+            scan(R("ZX", 256 * i, 256 * i + 256), m96, R("ZZ", 256 * i, 256 * i + 256), OP.mult, OP.add)
+            for h in H:
+                mm(R(bank, 96 * h, 96 * h + 96), R("ZX", 256 * i + 128 * h, 256 * i + 128 * h + 128), R("IDf"))
+        tt(R("mk"), R("b6", 0, 192), R("fp"), OP.is_equal)
+        tt(R(IC), R("b5", 0, 192), R("mk"), OP.mult)
+        if not last:
+            send(IC, [(dn1, "inA", "rA"), (up1, "inB", "rB")])
+        else:
+            send(IC, [(dn2, "inC", "rC")])
+        act(R("zr"), R("b4", 0, 192), AF.Identity, -4096.0)
+        tt_scatter(IND(RC, 0, 384, "LS", 12, 24), R("zr"), R("mRa"), OP.mult)
+        tt(R(MR), R(RC, 0, 192), R(mb), OP.max)
+        if not last:
+            send(MR, [(up2, "inM", "rR")])
+        tt(R("ox"), R("bf"), R("b6", 192, 384), OP.add)
+        ts(R("oy"), R("ox"), 192.0, OP.is_lt)
+        tt(R("ov"), R("ox"), R("oy"), OP.mult)
+        cp_scatter(IND("ow", 0, 4288, "LS", 0, 12), R("ov"))
+        if last:
+            dma("g", [((T.yown[:], []), (T.ow[0:128:16, 0:4096], [("ow", 0, 4096)]))])
+            return
+        cp_scatter(IND("X", 0, 4288, "LS", 0, 12), R("xg"))
+        tt(R("wf"), R("b6", 192, 384), R("ff"), OP.mult)
+        act(R("wg"), R("wf"), acc=R("wc"))
+        act(R("wb"), R("wc"))
+        mm(A("b7", 48, 49), R("oneB"), R("wb"))
+        ts(R("wi"), A("b7", 48, 49), 0.0625, OP.mult)
+        ts(R("wj"), R("wi"), 63, OP.bitwise_and)
+        ts(R("wk"), R("wj"), 1024.0, OP.mult)
+
+    def merged(old, new, words):
+        tt(R("mv"), R(old), R(new), OP.max)
+        ts(R(words), R("mv"), 4095, OP.bitwise_and)
+
+    play(0)
+    landed("inA", "rA", n16 // 2)
+    landed("inB", "rB", n16 // 2)
+    landed("inM", "rR", n16)
+    merged("inM", "inB", "mw")
+    cp(R("oI1"), R("mw"))
+    merged("MR0", "inA", "mi32")
+    cp(R("oR1"), R("mi32"))
+    cp(R("mb1"), R("mi32"))
+    ts(R("thA"), R("thA"), R("wk"), OP.add)
+    play(1)
+    landed("inC", "rC", n16)
+    merged("MR1", "inC", "mi32")
+    cp(R("yo"), R("mi32"))
+    dma("s", [((T.ym[:], []), R("yo"))])
+    for q in ("v", "a", "p", "g"):
+        g.wait_ge(S["q" + q], count[q])
+    for sem, val in loc_done:
+        g.wait_ge(S[sem], val)
+    g.wait_ge(S["d%d" % (ndma[0] - 2)], 16)
+    g.sync.wait_ge(S["d%d" % (ndma[0] - 1)], 16)

@@ -14,12 +14,13 @@ OWN_TILES = {
     U16: "oR0:192 oI0:192",
 }
 POOLS = {
-    F32: "pf:1 pp1:1 p15:1 p16:1 cc:128 kk:256 c16:12 IDf:96/96 dA:256/96 B6:6/96 K64:256/96 oneF:96/8 aC:24 TI:256/96 TR:256/96 T2:256/96 "
-         "PI:512/96 PN:512/96 KI:1024/96 FI:1024/96 KR:1024/96 FR:1024/96 KD:256/96 FD:256/96 t16:16/96 kfl:48/96 dk:16/96 dw:16/96 "
+    F32: "pf:1 pp1:1 p15:1 p16:1 cc:128 kk:256 c16:12 IDf:8/8 dA:256/96 B6:6/96 oneF:96/8 aC:24 Q1:256/96 Q23:512/96 "
+         "KI:1024/96 FI:1024/96 KR:768/96 FR:1024/96 FD:256/96 t16:16/96 kfl:48/96 dk:16/96 dw:16/96 "
          "ZS:256/96 SXm:256/96 SW:24 sI:192 sR:192 du:12 f2:24 l1:24 l2:24 l3:24 fp:192 mRa:192 ZL:512/96 LX:512/96 thA:16/96 w4:64/96 "
-         "mk:192 s1:64/96 s2:64/96 s5:32/96 ZZ:512/96 ZX:512/96 zr:192 wc:1 wk:1/96 thD:8/8 thf:1/8 mb0:192 mb1:192",
-    BF: "BI1:8 BI2:8 ID:128 dW:192 LT:192 j64:128/1 one1:128/1 oneB:96 HL:384 bf:192 bd:192 bs:192 ZW:192 bx:192 ff:192 ZR:256/96 RX:256/96 "
-        "FM:512/96 CN:512/96 ZK:512/96 KX:512/96 ox:192 oy:192 ov:192 xg:192 wf:192 wg:192 wb:1 V0:192",
+         "mk:192 s1:64/96 s2:64/96 zr:192 wc:1 wk:1/96 thD:8/8 thf:1/8 mb0:192 mb1:192",
+    BF: "BI1:8 BI2:8 BN1:8 BN2:8 ID:128 IDn:128 ID2:128 ID64:128 dW:192 LT:192 j64:256/1 j128:256/1 one1:128/1 oneB:96 HL:384 bf:192 bd:192 bs:192 "
+        "ZW:192 bx:192 ff:192 ZR:256/96 RX:256/96 FM:512/96 CN:512/96 ZK:512/96 KX:512/96 ZZ:1024/96 ZX:1024/96 ox:192 oy:192 ov:192 xg:192 "
+        "wf:192 wg:192 wb:1 V0:192",
     I32: "pI:1 pJ:1 CiI:192 CiR:192 HL32:384 eD:16/96 fD:16/96 eI:48/96 e63:32/96 kc:48/96 n32:192 s3:64/96 s4:64/96 wi:1/96 wj:1/96 mw:192 mv:192 a32:192",
     U16: "oI1:192 oR1:192 sL:12 nL:192 bU:192 Lb:12 LS:24 aU:192",
 }
@@ -229,7 +230,7 @@ def rank_program(g, core, T, topo):
     cp(R("oR0"), R("mi32"))
     send("oR0", [(up1, "oI0", "rM")])
     landed("oI0", "rM", n16)
-    for name, c in (("CZR", 0), ("EQ", 0), ("meq", 1), ("RC0", 0), ("RC1", 0)):
+    for name, c in (("CZR", 0), ("EQ", 0), ("meq", 1), ("ZR", 0), ("ZL", 0), ("ZK", 0), ("RC0", 0), ("RC1", 0)):
         iota(R(name), [[0, SHAPE[name][1]]], c)
     iota(R("FW", 0, 4096), [[0, 4096]], 1)
     iota(R("FW", 4096, 4288), [[0, 192]], 0)
@@ -239,11 +240,13 @@ def rank_program(g, core, T, topo):
     ts(R("pJ"), R("pI"), 4, OP.arith_shift_right)
     cp(R("p16"), R("pJ"))
     ts(R("ID"), R("cc"), R("pf"), OP.is_equal)
-    ts(R("BI1"), R("cc", 0, 8), R("p16"), OP.is_equal, 1024.0, OP.mult)
-    ts(R("BI2"), R("cc", 0, 8), R("p16"), OP.is_equal, 2048.0, OP.mult)
+    for name, c in (("BI1", 1024.0), ("BI2", 2048.0), ("BN1", -1024.0), ("BN2", -2048.0)):
+        ts(R(name), R("cc", 0, 8), R("p16"), OP.is_equal, c, OP.mult)
+    for name, c in (("IDn", -1.0), ("ID2", 2.0), ("ID64", 64.0)):
+        ts(R(name), R("ID"), c, OP.mult)
     ms(R("one1"), 1.0)
-    ts(R("K64"), A("kk"), 64.0, OP.mult)
-    cp(R("j64"), R("K64", 0, 128, 1, 1))
+    ts(R("j64"), R("kk", 0, 256, 1, 1), 64.0, OP.mult)
+    ts(R("j128"), R("kk", 0, 256, 1, 1), 128.0, OP.mult)
     ms(R("mB"), 0.0)
     ms(R("mB", 0, 1024, 16), BIG)
     ms(R("ZS"), 0.0)
@@ -252,30 +255,29 @@ def rank_program(g, core, T, topo):
     cp(R("ob"), R("od"))
     dma("s", [((T.odr[:], [("odr", 0, 4096)]), R("ob"))])
     dma("s", [((T.ow[r:128:16, 0:4096], [("ow", 0, 4096)]), (T.odr[:], [("odr", 0, 4096)])) for r in range(16)])
-    ts(R("IDf"), A("cc", 0, 96), R("pf", p=96), OP.is_equal)
+    ts(R("IDf"), R("cc", 0, 8, 1, 8), R("pf", p=8), OP.is_equal)
     ts(R("dW"), R("kk", 0, 192), R("p15"), OP.is_equal)
     ts(R("LT"), R("kk", 0, 192), R("p15"), OP.is_ge, 1000.0, OP.mult)
     ms(R("ZW"), 0.0)
+    ms(R("ZZ"), 0.0)
+    cp(R("aU"), R("a32"))
+    ts(R("aC", 0, 12), R("c16"), R("p15"), OP.add, 4096.0, OP.add)
+    ts(R("aC", 12, 24), R("c16"), R("p15"), OP.add, 192.0, OP.add)
+    ts(R("pp1"), R("p15"), 1.0, OP.add)
 
-    def late_constants():
-        for name in ("ZK", "ZR", "ZL", "ZZ"):
-            ms(R(name), 0.0)
-        cp(R("aU"), R("a32"))
-        ts(R("pp1"), R("p15"), 1.0, OP.add)
-        ts(R("aC", 0, 12), R("c16"), R("p15"), OP.add, 4096.0, OP.add)
-        ts(R("aC", 12, 24), R("c16"), R("p15"), OP.add, 192.0, OP.add)
-        ms(R("meq", 0, 1936, 176), 0.0)
-        ms(R("meq", 1936, 2128, 16), 0.0)
-        ms(R("X", 4096, 4288), 0.0)
-        ms(R("ow", 4096, 4288), 0.0)
-        ms(R("oneB"), 1.0)
+    def thresholds():
         ms(R("oneF"), 1.0)
-        cp(R("mb0"), R("mi32"))
         cp(R("thf"), R("thi"))
-        ts(R("thD"), R("IDf", 0, 8, 1, 8), R("thf"), OP.mult)
+        ts(R("thD"), R("IDf"), R("thf"), OP.mult)
         mm(R("b6", 0, 8, 1, 96), R("oneF"), R("thD"))
         for h in H:
             ts(R("thA", 8 * h, 8 * h + 8), A("b6", 0, 8), 1024.0, OP.mult)
+
+    def late_constants():
+        ms(R("X", 4096, 4288), 0.0)
+        ms(R("ow", 4096, 4288), 0.0)
+        ms(R("oneB"), 1.0)
+        cp(R("mb0"), R("mi32"))
 
     def half(name, h, step=1):
         return R(name, 1536 * h, 1536 * h + 1536, step)
@@ -283,9 +285,34 @@ def rank_program(g, core, T, topo):
     def gather(v, off, h):
         act(half(v, h), IND("X", 0, 4096, off, 96 * h, 96 * h + 96))
 
-    def group_sum(bank, src, w, h):
+    def begin(bank):
+        mm(A(bank, 0, 256), R("one1", 0, 96), R("j64"), True, False)
+
+    def group_sum(bank, src, w, h, stop=False):
         for k in range(16):
-            mm(A(bank, 128 * h + k, 128 * h + 128, 16), R(src, 1536 * h + k, 1536 * h + 1536, 16), R(w))
+            mm(A(bank, 128 * h + k, 128 * h + 128, 16), R(src, 1536 * h + k, 1536 * h + 1536, 16), R(w), False, stop and k == 15)
+
+    def digits(bank, at, i, h, w, start=False, stop=False):
+        mm(A(bank, at + 128 * h, at + 128 * h + 128), R("HL", 192 * i + 96 * h, 192 * i + 96 * h + 96), R(w), start, stop)
+
+    def split(m32):
+        ts(R("HL32", 0, 192), R(m32), 6, OP.arith_shift_right)
+        ts(R("HL32", 192, 384), R(m32), 63, OP.bitwise_and)
+        cp(R("HL"), R("HL32"))
+
+    def payload(wide):
+        for h in H:
+            digits("b2", 0, 1, h, "ID", True, False)
+            digits("b2", 0, 0, h, "IDn", False, True)
+        act(R("Q1"), A("b2", 0, 256))
+        for i in range(2 if wide else 1):
+            mm(A("b4", 256 * i, 256 * i + 256), R("one1", 0, 96), R("j128"), True, False)
+            for h in H:
+                digits("b4", 256 * i, 0, h, "ID" if i else "ID2", False, h == 1 and not i)
+                if i:
+                    digits("b4", 256 * i, 1, h, "ID", False, h == 1)
+        n = 512 if wide else 256
+        act(R("Q23", 0, n), A("b4", 0, n))
 
     def extremes(v, mx, mn, h):
         scan(half(mx, h), R("m01"), half(v, h), OP.mult, OP.max)
@@ -296,22 +323,12 @@ def rank_program(g, core, T, topo):
         ts(R(ci), R(s), 0.5, OP.mult, -0.25, OP.add)
         cp(R(cz, 0, 3072, 16), R(ci))
 
+    def spread(cx, cz, h):
+        scan(half(cx, h), R("m01"), half(cz, h), OP.mult, OP.add)
+
     def larger(v, first, cx, c0, d, h):
         tt(half(v, h, 16), first, half(c0, h, 16), OP.max)
         scan(half(d, h), half(cx, h), half(v, h), OP.min, OP.max)
-
-    def split(m32):
-        ts(R("HL32", 0, 192), R(m32), 6, OP.arith_shift_right)
-        ts(R("HL32", 192, 384), R(m32), 63, OP.bitwise_and)
-        cp(R("HL"), R("HL32"))
-
-    def payload(dst):
-        for i in range(2):
-            for h in H:
-                o = A("b4", 256 * i + 128 * h, 256 * i + 128 * h + 128)
-                mm(o, R("HL", 192 * i + 96 * h, 192 * i + 96 * h + 96), R("ID"), True, False)
-                mm(o, R("one1", 0, 96), R("j64"), False, True)
-        act(R(dst), A("b4"))
 
     def seg(f, lo, hi):
         return A(f, lo + 15, hi, 16)
@@ -322,37 +339,37 @@ def rank_program(g, core, T, topo):
         last = t == 1
         m96 = R("m01", 0, 256, 1, 96)
         m96x2 = R("m01", 0, 512, 1, 96)
+        mB1 = A("mB", 0, 256)
         if t == 0:
+            thresholds()
             cp(R("mw"), R(oI))
-        for h in H:
-            gather("VI", oI, h)
+        gather("VI", oI, 0)
+        act(R("VI", 1536, 2304), IND("X", 0, 4096, oI, 96, 144))
+        cp(R("VI", 2304, 3072), IND("X", 0, 4096, oI, 144, 192))
         split("mw")
         for h in H:
             extremes("VI", "XI", "NI", h)
-        payload("PI")
+        begin("b0")
+        for h in H:
+            digits("b0", 0, 0, h, "ID")
+        payload(False)
         gather("VR", oR, 0)
         for h in H:
-            group_sum("b2", "VI", "BI1", h)
-        act(R("TI"), A("b2", 0, 256))
+            group_sum("b0", "VI", "BN1", h)
         gather("VR", oR, 1)
         centres("XI", "NI", "sI", "CiI", "CZI")
         for h in H:
-            scan(half("CXI", h), R("m01"), half("CZI", h), OP.mult, OP.add)
+            spread("CXI", "CZI", h)
             larger("VI", half("VI", h, 16), "CXI", "CZI", "DA", h)
-            group_sum("b0", "DA", "BI2", h)
-        for h in H:
-            group_sum("b2", "VR", "BI1", h)
-        if t == 0:
-            late_constants()
+            group_sum("b0", "DA", "BI2", h, h == 1)
         extremes("VR", "XR", "NR", 0)
-        u = A("b3", 0, 256)
-        tt(u, A("b0", 0, 256), R("TI"), OP.subtract)
-        tt(R("KI", 0, 256), u, R("PI", 0, 256), OP.add)
-        tt(R("KI", 256, 512), u, R("PI", 256, 512), OP.add)
-        tt(R("KI", 512, 768), R("PI", 0, 256), u, OP.subtract)
-        scan(R("FI", 0, 768), R("mB", 0, 768, 1, 96), R("KI", 0, 768), OP.add, OP.min)
-        cp(R("eI"), seg("FI", 0, 768))
+        u, a0 = A("b3", 0, 256), A("b0", 0, 256)
+        scan(R("FI", 0, 256), mB1, a0, OP.add, OP.min)
+        tt(R("KI", 0, 256), a0, R("Q1"), OP.add)
+        scan(R("FI", 256, 512), mB1, R("KI", 0, 256), OP.add, OP.min)
+        cp(R("eI", 0, 32), seg("FI", 0, 512))
         ts(R("e63"), R("eI", 0, 32), 63, OP.bitwise_and)
+        tt(R("KI", 512, 768), R("Q23", 0, 256), a0, OP.subtract)
         ts(R("t16"), R("e63", 0, 16), 64.0, OP.mult)
         tt(R("ZS", 0, 256, 16), R("t16"), R("e63", 16, 32), OP.add)
         scan(u, m96, R("ZS"), OP.mult, OP.add)
@@ -360,12 +377,14 @@ def rank_program(g, core, T, topo):
         for h in H:
             mm(R("b7", 6 * h, 6 * h + 6), R("SXm", 128 * h, 128 * h + 128), R("B6"))
         cp(R("sL"), R("b7", 0, 12))
+        begin("b5")
+        for h in H:
+            group_sum("b5", "VR", "BI1", h)
         cp(R("nL"), IND("nbw", 0, 4096, "sL", 0, 12))
         act(R("SW", 0, 12), R("b7", 0, 12))
         for h in H:
             gather("V2", "nL", h)
             act(R("V0", 96 * h, 96 * h + 96), half("V2", h, 16))
-        act(R("TR"), A("b2", 0, 256))
         cp(R("bf"), IND("ow", 0, 4096, "sL", 0, 12))
         cp(R("bU"), R("bf"))
         mm(R("b6", 0, 192), R("ID"), R("bf"), True, False)
@@ -377,12 +396,23 @@ def rank_program(g, core, T, topo):
             act(half("CXB", h), IND("CRc", 0, 192, "bU", 96 * h, 96 * h + 96))
         cp(R("n32"), R("nL"))
         split("n32")
-        payload("PN")
+        for bank in ("b0", "b1"):
+            begin(bank)
+            for h in H:
+                digits(bank, 0, 0, h, "ID")
         for h in H:
-            group_sum("b2", "V2", "BI1", h)
-        act(R("T2"), A("b2", 0, 256))
-        for h in H:
-            act(half("CXR", h), IND("CRc", 0, 192, "aU", 96 * h, 96 * h + 96))
+            for bank in ("b0", "b1"):
+                group_sum(bank, "V2", "BN1", h)
+        scan(R("FI", 512, 768), mB1, R("KI", 512, 768), OP.add, OP.min)
+        payload(True)
+        act(half("CXR", 1), IND("CRc", 0, 192, "aU", 96, 192))
+        cp(R("eI", 32, 48), seg("FI", 512, 768))
+        ts(R("kc"), R("eI"), 6, OP.arith_shift_right, 15, OP.bitwise_and)
+        cp(R("kfl"), R("kc"))
+        tt(R("dk"), R("kfl", 32, 48), R("kfl", 0, 16), OP.subtract)
+        if t == 0:
+            ms(R("meq", 0, 1936, 176), 0.0)
+            ms(R("meq", 1936, 2128, 16), 0.0)
         tt(R("bd"), R("bf"), R("dW"), OP.mult)
         scan(R("bs"), R("m01", 0, 192), R("bd"), OP.mult, OP.add)
         cp(R("SW", 12, 24), R("bs", 15, 192, 16))
@@ -404,48 +434,36 @@ def rank_program(g, core, T, topo):
         cp(R("LS"), R("l3"))
         for h in H:
             larger("V2", R("V0", 96 * h, 96 * h + 96), "CXI", "CZI", "DA", h)
-            group_sum("b0", "DA", "BI2", h)
-        for h in H:
-            larger("VR", half("VR", h, 16), "CXR", "CZR", "DB", h)
-            group_sum("b1", "DB", "BI2", h)
+            group_sum("b0", "DA", "BI2", h, h == 1)
         act(R("ff"), IND("FW", 0, 4288, "LS", 0, 12))
         act(R("fp"), R("ff"), AF.Identity, -1.0, R("pp1"))
         if not last:
             act(R("xg"), IND("X", 0, 4096, "sL", 0, 12), AF.Relu, -16.0)
-        ur = A("b3", 256, 512)
-        tt(ur, A("b1", 0, 256), R("TR"), OP.subtract)
-        tt(R("KD"), R("K64"), ur, OP.subtract)
-        scan(R("FD"), R("mB", 0, 256, 1, 96), R("KD"), OP.add, OP.min)
-        cp(R("eD"), seg("FD", 0, 256))
-        ts(R("fD"), R("eD"), 6, OP.arith_shift_right, 15, OP.bitwise_and)
-        cp(R("ZR", 0, 256, 16), R("fD"))
-        scan(R("RX"), m96, R("ZR"), OP.mult, OP.add)
-        for h in H:
-            mm(R("b6", 96 * h, 96 * h + 96), R("RX", 128 * h, 128 * h + 128), R("ID", 0, 96, 1, 96))
-        ts(R("mR"), R("b6", 0, 192), R("p15"), OP.is_equal)
-        act(R("mRa"), IND("mR", 0, 192, "Lb", 0, 12))
         for h in H:
             larger("V2", R("V0", 96 * h, 96 * h + 96), "CXB", "CXB", "DB", h)
-            group_sum("b1", "DB", "BI2", h)
+            group_sum("b1", "DB", "BI2", h, h == 1)
         for i, cz in ((0, "CZI"), (1, "CXB")):
             for h in H:
                 mm(A("b7", 16 + 16 * i + 8 * h, 24 + 16 * i + 8 * h), half(cz, h, 16), R("BI1"))
-        ui = A("b3", 0, 256)
-        tt(ui, A("b0", 0, 256), R("T2"), OP.subtract)
-        hi, lo = R("PN", 0, 256), R("PN", 256, 512)
-        tt(R("KI", 0, 256), ui, hi, OP.add)
-        tt(R("KI", 256, 512), hi, ui, OP.subtract)
-        tt(R("KI", 512, 768), ui, lo, OP.add)
-        tt(R("KI", 768, 1024), lo, ui, OP.subtract)
-        ts(R("kc"), R("eI"), 6, OP.arith_shift_right, 15, OP.bitwise_and)
-        cp(R("kfl"), R("kc"))
-        tt(R("dk"), R("kfl", 32, 48), R("kfl", 0, 16), OP.subtract)
-        scan(R("FI"), A("mB"), R("KI"), OP.add, OP.min)
+        if t == 0:
+            late_constants()
+        spread("CXR", "CZR", 0)
+        for h in H:
+            larger("VR", half("VR", h, 16), "CXR", "CZR", "DA", h)
+            group_sum("b5", "DA", "BN2", h, h == 1)
+        ui, ur = a0, A("b1", 0, 256)
+        q1, q2, q3 = R("Q1"), R("Q23", 0, 256), R("Q23", 256, 512)
+        scan(R("FI", 0, 256), mB1, ui, OP.add, OP.min)
+        tt(R("KI", 256, 512), q2, ui, OP.subtract)
+        tt(R("KI", 512, 768), ui, q1, OP.add)
+        tt(R("KI", 768, 1024), q3, ui, OP.subtract)
+        scan(R("FI", 256, 1024), A("mB", 256, 1024), R("KI", 256, 1024), OP.add, OP.min)
+        if not last:
+            cp_scatter(IND("X", 0, 4288, "LS", 0, 12), R("xg"))
         for i in (0, 1):
             tt(R("ZL", 256 * i, 256 * i + 256, 16), A("b7", 16 + 16 * i, 32 + 16 * i), R("thA"), OP.add)
         scan(R("LX"), m96x2, R("ZL"), OP.mult, OP.add)
         tt(R("FM", 0, 256), ui, R("LX", 0, 256), OP.is_lt)
-        tt(ur, A("b1", 0, 256), R("T2"), OP.subtract)
         tt(R("FM", 256, 512), ur, R("LX", 256, 512), OP.is_lt)
         scan(R("CN"), m96x2, R("FM"), OP.mult, OP.add)
         tt(R("w4", 0, 16), seg("CN", 0, 256), seg("CN", 256, 512), OP.is_gt)
@@ -454,43 +472,54 @@ def rank_program(g, core, T, topo):
         act(R("ZK", 256, 512, 16), R("w4", 0, 16))
         tt(R("dw"), R("dk"), R("w4", 0, 16), OP.mult)
         tt(R("ZK", 0, 256, 16), R("dw"), R("kfl", 0, 16), OP.add)
-        tt(R("KR", 0, 256), hi, ur, OP.subtract)
-        tt(R("KR", 256, 512), ur, hi, OP.add)
+        tt(R("KR", 0, 256), q2, ur, OP.subtract)
+        scan(R("FR", 256, 512), mB1, ur, OP.add, OP.min)
         scan(R("KX"), m96x2, R("ZK"), OP.mult, OP.add)
+        tt(R("KR", 256, 512), q3, ur, OP.subtract)
+        tt(R("KR", 512, 768), ur, q1, OP.add)
+        scan(R("FR", 0, 256), mB1, R("KR", 0, 256), OP.add, OP.min)
+        scan(R("FR", 512, 1024), A("mB", 0, 512), R("KR", 256, 768), OP.add, OP.min)
+        scan(R("FD"), mB1, A("b5", 0, 256), OP.add, OP.min)
+        cp(R("eD"), seg("FD", 0, 256))
+        ts(R("fD"), R("eD"), 6, OP.arith_shift_right, 15, OP.bitwise_and)
+        cp(R("ZR", 0, 256, 16), R("fD"))
+        scan(R("RX"), m96, R("ZR"), OP.mult, OP.add)
+        for h in H:
+            mm(R("b6", 96 * h, 96 * h + 96), R("RX", 128 * h, 128 * h + 128), R("ID", 0, 96, 1, 96))
+        ts(R("mR"), R("b6", 0, 192), R("p15"), OP.is_equal)
+        act(R("mRa"), IND("mR", 0, 192, "Lb", 0, 12))
         for i in range(4):
             mm(R("b6", 96 * i, 96 * i + 96), R("KX", 128 * i, 128 * i + 128), R("ID", 0, 96, 1, 96))
-        tt(R("KR", 512, 768), lo, ur, OP.subtract)
-        tt(R("KR", 768, 1024), ur, lo, OP.add)
-        scan(R("FR"), A("mB"), R("KR"), OP.add, OP.min)
         tt(R("s1"), seg("FI", 0, 1024), seg("FR", 0, 1024), OP.subtract)
         tt(R("s2"), R("s1"), R("w4"), OP.mult)
         tt(R("s3"), R("s2"), seg("FR", 0, 1024), OP.add)
         ts(R("s4"), R("s3"), 63, OP.bitwise_and)
-        ts(R("s5"), R("s4", 0, 32), 64.0, OP.mult, 8192.0, OP.add)
-        tt(R("ZZ", 0, 512, 16), R("s5"), R("s4", 32, 64), OP.add)
-        for i, bank in ((0, "b5"), (1, "b4")):
-            scan(R("ZX", 256 * i, 256 * i + 256), m96, R("ZZ", 256 * i, 256 * i + 256), OP.mult, OP.add)
+        ts(R("ZZ", 0, 512, 16), R("s4", 0, 32), 128.0, OP.add)
+        cp(R("ZZ", 512, 1024, 16), R("s4", 32, 64))
+        for i, bank in ((0, "b5"), (1, "b4")) if last else ((1, "b4"), (0, "b5")):
+            for d in (0, 512):
+                scan(R("ZX", d + 256 * i, d + 256 * i + 256), m96, R("ZZ", d + 256 * i, d + 256 * i + 256), OP.mult, OP.add)
             for h in H:
-                mm(R(bank, 96 * h, 96 * h + 96), R("ZX", 256 * i + 128 * h, 256 * i + 128 * h + 128), R("IDf"))
+                for d, w in ((0, "ID64"), (512, "ID")):
+                    mm(R(bank, 96 * h, 96 * h + 96), R("ZX", d + 256 * i + 128 * h, d + 256 * i + 128 * h + 128), R(w, 0, 96, 1, 96), d == 0, d > 0)
+        tt(R("ox"), R("bf"), R("b6", 192, 384), OP.add)
+        ts(R("oy"), R("ox"), 192.0, OP.is_lt)
+        tt(R("ov"), R("ox"), R("oy"), OP.mult)
+        act(R("zr"), R("b4", 0, 192), AF.Identity, -4096.0)
         tt(R("mk"), R("b6", 0, 192), R("fp"), OP.is_equal)
         tt(R(IC), R("b5", 0, 192), R("mk"), OP.mult)
         if not last:
             send(IC, [(dn1, "inA", "rA"), (up1, "inB", "rB")])
         else:
             send(IC, [(dn2, "inC", "rC")])
-        act(R("zr"), R("b4", 0, 192), AF.Identity, -4096.0)
         tt_scatter(IND(RC, 0, 384, "LS", 12, 24), R("zr"), R("mRa"), OP.mult)
         tt(R(MR), R(RC, 0, 192), R(mb), OP.max)
         if not last:
             send(MR, [(up2, "inM", "rR")])
-        tt(R("ox"), R("bf"), R("b6", 192, 384), OP.add)
-        ts(R("oy"), R("ox"), 192.0, OP.is_lt)
-        tt(R("ov"), R("ox"), R("oy"), OP.mult)
         cp_scatter(IND("ow", 0, 4288, "LS", 0, 12), R("ov"))
         if last:
             dma("g", [((T.yown[:], []), (T.ow[0:128:16, 0:4096], [("ow", 0, 4096)]))])
             return
-        cp_scatter(IND("X", 0, 4288, "LS", 0, 12), R("xg"))
         tt(R("wf"), R("b6", 192, 384), R("ff"), OP.mult)
         act(R("wg"), R("wf"), acc=R("wc"))
         act(R("wb"), R("wc"))
@@ -507,10 +536,10 @@ def rank_program(g, core, T, topo):
     landed("inA", "rA", n16 // 2)
     landed("inB", "rB", n16 // 2)
     landed("inM", "rR", n16)
-    merged("inM", "inB", "mw")
-    cp(R("oI1"), R("mw"))
     merged("MR0", "inA", "mi32")
     cp(R("oR1"), R("mi32"))
+    merged("inM", "inB", "mw")
+    cp(R("oI1"), R("mw"))
     cp(R("mb1"), R("mi32"))
     ts(R("thA"), R("thA"), R("wk"), OP.add)
     play(1)

from concourse.bass import DstId, RemoteDMATransfer
from concourse.mybir import AluOpType, ActivationFunctionType

OP = AluOpType
AF = ActivationFunctionType
F32, BF, I32, U16 = "float32", "bfloat16", "int32", "uint16"
BIG = float(2 ** 26)

OWN_TILES = {
    F32: "IC0:192 IC1:192 RC0:384 RC1:384 MR0:192 MR1:192 inA:192 inB:192 inM:192 inC:192 yo:192",
    BF: "X:4288 ow:4288 FW:4288 ob:256 VI:3072 VR:3072 V2:3072 XI:3072 NI:3072 XR:3072 NR:3072 CZI:3072 CZR:3072 "
        "CXI:3072 CXR:3072 CXB:3072 DA:3072 DB:3072 m01:1536 m512:1536 mB:1024 meq:2128 EQ:2128 EC:2128 CRc:192 mR:192",
    I32: "nbw:4096 od:256 mi32:192 thi:1",
    U16: "oR0:192 oI0:192",
}
POOLS = {
    F32: "pf:1 pp1:1 p15:1 p16:1 cc:128 kk:256 c16:12 IDf:8/8 dA:256/96 B6:6/96 oneF:96/8 aC:24 Q1:256/96 Q23:512/96 "
         "KI:1024/96 FI:1024/96 KR:768/96 FR:1024/96 FD:256/96 t16:16/96 kfl:48/96 dk:16/96 dw:16/96 "
         "ZS:256/96 SXm:256/96 SW:24 sI:192 sR:192 du:12 f2:24 l1:24 l2:24 l3:24 fp:192 mRa:192 ZL:512/96 LX:512/96 thA:16/96 w4:64/96 "
         "mk:192 s1:64/96 s2:64/96 zr:192 wc:1 wk:1/96 thD:8/8 thf:1/8 mb0:192 mb1:192",
    BF: "BI1:8 BI2:8 BN1:8 BN2:8 ID:128 IDn:128 ID2:128 ID64:128 dW:192 LT:192 j64:256/1 j128:256/1 one1:128/1 oneB:96 HL:384 bf:192 bd:192 bs:192 "
        "ZW:192 bx:192 ff:192 ZR:256/96 RX:256/96 FM:512/96 CN:512/96 ZK:512/96 KX:512/96 ZZ:1024/96 ZX:1024/96 ox:192 oy:192 ov:192 xg:192 "
        "wf:192 wg:192 wb:1 V0:192",
    I32: "pI:1 pJ:1 CiI:192 CiR:192 HL32:384 eD:16/96 fD:16/96 eI:48/96 e63:32/96 kc:48/96 n32:192 s3:64/96 s4:64/96 wi:1/96 wj:1/96 mw:192 mv:192 a32:192",
    U16: "oI1:192 oR1:192 sL:12 nL:192 bU:192 Lb:12 LS:24 aU:192",
}
SCRATCH, SHAPE, PLACE = {}, {}, {}
for _d, _names in OWN_TILES.items():
    for _n in _names.split():
        _n, _w = _n.split(":")
        _p = 8 if _n == "thi" else 128
        SCRATCH[_n] = ("sbuf", [_p, int(_w)], _d)
        SHAPE[_n], PLACE[_n] = (_p, int(_w)), (_n, 0)
for _d, _names in POOLS.items():
    _at = 0
    for _n in _names.split():
        _n, _w = _n.split(":")
        _w = (_w + "/128").split("/")
        SHAPE[_n], PLACE[_n] = (int(_w[1]), int(_w[0])), ("pool_" + _d, _at)
        _at += -(-int(_w[0]) // 16) * 16
    SCRATCH["pool_" + _d] = ("sbuf", [128, _at], _d)
SCRATCH["odr"] = ("dram", [8, 4096], BF)
PSUM = ["b%d" % _i for _i in range(8)]
for _n in PSUM:
    SCRATCH[_n] = ("psum", [128, 512], F32)
    SHAPE[_n], PLACE[_n] = (128, 512), (_n, 0)
SEMAPHORES = ["qv", "qa", "qp", "qg"] + ["d%d" % i for i in range(16)] + ["rM", "rA", "rB", "rR", "rC"] + ["l%d" % i for i in range(5)]


def rank_program(g, core, T, topo):
    rank = T.rank_of(core)
    if rank is None:
        return
    n_ranks = len(T.cores)
    S = T.sem
    queue = {"v": g.vector, "a": g.scalar, "p": g.tensor, "g": g, "s": g.sync}
    count = {"v": 0, "a": 0, "p": 0, "g": 0}
    known = {"v": {}, "a": {}, "p": {}, "g": {}, "s": {}}
    snap = {}
    log = {}
    ndma = [0]

    def R(name, lo=0, hi=None, step=1, p=None):
        shape = SHAPE[name]
        hi = shape[1] if hi is None else hi
        p = shape[0] if p is None else p
        buf, at = PLACE[name]
        ap = T[buf][0:p, at + lo:at + hi:step] if step > 1 else T[buf][0:p, at + lo:at + hi]
        return (ap, [(name, lo, hi)])

    def A(name, lo=0, hi=None, step=1):
        return R(name, lo, hi, step, 96)

    def IND(win, lo, hi, off, c0, c1):
        buf, at = PLACE[off]
        return (T[win][:, lo:hi].indirect(T[buf][:, at + c0:at + c1]), [(win, lo, hi), (off, c0, c1)])

    def learn(q, sem, val):
        k = known[q]
        for s2, v2 in snap.get((sem, val), {}).items():
            k[s2] = max(k.get(s2, 0), v2)
        k[sem] = max(k.get(sem, 0), val)

    def need(q, reads, writes, skip_own=False):
        deps = {}
        for lst, wr in ((reads, False), (writes, True)):
            for name, lo, hi in lst:
                for e in log.get(name, ()):
                    if name in PSUM and e[1] != q:
                        hit = True
                    else:
                        hit = (wr or e[0]) and e[4] < hi and lo < e[5]
                    if hit and not (skip_own and e[1] == q):
                        deps[e[2]] = max(deps.get(e[2], 0), e[3])
        for sem, val in sorted(deps.items(), key=lambda d: -len(snap.get(d, {}))):
            if known[q].get(sem, 0) < val:
                queue[q].wait_ge(S[sem], val)
                learn(q, sem, val)

    def note(q, sem, val, reads, writes):
        for lst, wr in ((reads, False), (writes, True)):
            for name, lo, hi in lst:
                old = log.setdefault(name, [])
                if wr:
                    old[:] = [e for e in old if not (lo <= e[4] and e[5] <= hi)]
                old.append([wr, q, sem, val, lo, hi])

    def spans(refs):
        return [s for r in refs for s in r[1]]

    def emit(q, call, outs, ins, skip_own=False):
        rd, wr = spans(ins), spans(outs)
        need(q, rd, wr, skip_own)
        count[q] += 1
        sem = "q" + q
        call().then_inc(S[sem], 1)
        snap[(sem, count[q])] = dict(known[q])
        note(q, sem, count[q], rd, wr)

    def ind_out(o):
        return (o[0], o[1][:1]), (o[0], o[1][1:])

    def tt(o, a, b, op):
        emit("v", lambda: g.vector.tensor_tensor(o[0], a[0], b[0], op), [o], [a, b])

    def tt_scatter(o, a, b, op):
        w, l = ind_out(o)
        emit("v", lambda: g.vector.tensor_tensor(o[0], a[0], b[0], op), [w], [a, b, l])

    def ts(o, a, s1, op0, s2=None, op1=None):
        sc1 = s1[0] if isinstance(s1, tuple) else s1
        ins = [a] + ([s1] if isinstance(s1, tuple) else [])
        if op1 is None:
            emit("v", lambda: g.vector.tensor_scalar(o[0], a[0], sc1, None, op0), [o], ins)
        else:
            emit("v", lambda: g.vector.tensor_scalar(o[0], a[0], sc1, s2, op0, op1), [o], ins)

    def cp(o, a):
        emit("v", lambda: g.vector.tensor_copy(o[0], a[0]), [o], [a])

    def cp_scatter(o, a):
        w, l = ind_out(o)
        emit("v", lambda: g.vector.tensor_copy(o[0], a[0]), [w], [a, l])

    def ms(o, c):
        emit("v", lambda: g.vector.memset(o[0], c), [o], [])

    def scan(o, d0, d1, op0, op1):
        emit("v", lambda: g.vector.tensor_tensor_scan(o[0], d0[0], d1[0], 0.0, op0, op1), [o], [d0, d1])

    def act(o, a, func=AF.Copy, bias=0.0, scale=1.0, acc=None):
        ins = [a] + ([scale] if isinstance(scale, tuple) else [])
        sc = scale[0] if isinstance(scale, tuple) else scale
        if acc is None:
            emit("a", lambda: g.scalar.activation(o[0], a[0], func, bias=bias, scale=sc), [o], ins)
        else:
            emit("a", lambda: g.scalar.activation(o[0], a[0], func, bias=bias, scale=sc, accum_out=acc[0]), [o, acc], ins)

    def mm(o, l, r, start=True, stop=True):
        emit("p", lambda: g.tensor.matmul(o[0], l[0], r[0], start, stop), [o], [l, r], True)

    def iota(o, pat, base=0, cm=0, flag=True):
        kw = {"allow_small_or_imprecise_dtypes": True} if flag else {}
        emit("g", lambda: g.iota(o[0], pat, base, cm, **kw), [o], [])

    def dma(q, pairs):
        rd, wr = spans([b for a, b in pairs]), spans([a for a, b in pairs])
        need(q, rd, wr)
        sem = "d%d" % ndma[0]
        ndma[0] += 1
        for a, b in pairs:
            queue[q].dma_start(a[0], b[0]).then_inc(S[sem], 16)
        snap[(sem, 16 * len(pairs))] = dict(known[q])
        note("dma", sem, 16 * len(pairs), rd, wr)

    def ext(t):
        return (t[:], [])

    nloc = [0]
    loc_done = []

    def send(src, outs):
        need("g", [(src, 0, 192)], [])
        ls = "l%d" % nloc[0]
        nloc[0] += 1
        total = 0
        tr = []
        for i, (d, land, rs) in enumerate(outs):
            dst = T.cores[d]
            rid, pid, _ = topo.addr(dst)
            es = topo.engines(core, dst)
            m = len(es) // len(outs)
            es = es[i * m:(i + 1) * m]
            total += m
            tr.append((rid, pid, sum(1 << e for e in es), land, rs))
        if len(tr) == 1:
            rid, pid, mask, land, rs = tr[0]
            g.remote_dma(T[land][:], T[src][:], S[rs], S[ls], pid, rid, mask)
        else:
            g.remote_dma_fused([RemoteDMATransfer(dst_ids=[DstId(rid=rid, pnc=pid)], dma_engine_mask=mask, remote_sem=S[rs],
                                                  src=T[src][:], dst=T[land][:]) for rid, pid, mask, land, rs in tr], local_sem=S[ls])
        snap[(ls, total)] = dict(known["g"])
        note("rem", ls, total, [(src, 0, 192)], [])
        loc_done.append((ls, total))

    def landed(land, sem, val):
        note("rem", sem, val, [], [(land, 0, 192)])

    up1, up2 = (rank + 1) % n_ranks, (rank + 2) % n_ranks
    dn1, dn2 = (rank - 1) % n_ranks, (rank - 2) % n_ranks
    n16 = len(topo.engines(core, T.cores[up1]))
    H = (0, 1)

    dma("s", [(R("mi32"), ext(T.m0))])
    dma("s", [(R("X", 0, 4096), ext(T.x0))])
    dma("a", [(R("od"), ext(T.own0))])
    dma("a", [(R("thi"), ext(T.th))])
    dma("s", [(R("nbw"), ext(T.nb))])
    iota(R("pI"), [[0, 1]], 0, 1, False)
    iota(R("kk"), [[0, 16], [1, 16]])
    iota(R("cc"), [[1, 128]])
    iota(R("c16"), [[16, 12]])
    iota(R("a32"), [[1, 192]], 0, 0, False)
    ms(R("m01"), 1.0)
    ms(R("m01", 0, 1536, 16), 0.0)
    ms(R("m512"), 0.0)
    ms(R("m512", 0, 1536, 16), 512.0)
    for h in H:
        act(R("CZI", 1536 * h, 1536 * h + 1536), R("m01"), AF.Copy, 0.0, 0.0)
    cp(R("oR0"), R("mi32"))
    send("oR0", [(up1, "oI0", "rM")])
    landed("oI0", "rM", n16)
    for name, c in (("CZR", 0), ("EQ", 0), ("meq", 1), ("ZR", 0), ("ZL", 0), ("ZK", 0), ("RC0", 0), ("RC1", 0)):
        iota(R(name), [[0, SHAPE[name][1]]], c)
    iota(R("FW", 0, 4096), [[0, 4096]], 1)
    iota(R("FW", 4096, 4288), [[0, 192]], 0)
    ts(R("pJ"), R("pI"), 15, OP.bitwise_and)
    cp(R("p15"), R("pJ"))
    cp(R("pf"), R("pI"))
    ts(R("pJ"), R("pI"), 4, OP.arith_shift_right)
    cp(R("p16"), R("pJ"))
    ts(R("ID"), R("cc"), R("pf"), OP.is_equal)
    for name, c in (("BI1", 1024.0), ("BI2", 2048.0), ("BN1", -1024.0), ("BN2", -2048.0)):
        ts(R(name), R("cc", 0, 8), R("p16"), OP.is_equal, c, OP.mult)
    for name, c in (("IDn", -1.0), ("ID2", 2.0), ("ID64", 64.0)):
        ts(R(name), R("ID"), c, OP.mult)
    ms(R("one1"), 1.0)
    ts(R("j64"), R("kk", 0, 256, 1, 1), 64.0, OP.mult)
    ts(R("j128"), R("kk", 0, 256, 1, 1), 128.0, OP.mult)
    ms(R("mB"), 0.0)
    ms(R("mB", 0, 1024, 16), BIG)
    ms(R("ZS"), 0.0)
    ts(R("dA"), A("kk"), R("p15", p=96), OP.is_equal)
    ts(R("B6"), A("cc", 0, 6), R("p16", p=96), OP.is_equal)
    cp(R("ob"), R("od"))
    dma("s", [((T.odr[:], [("odr", 0, 4096)]), R("ob"))])
    dma("s", [((T.ow[r:128:16, 0:4096], [("ow", 0, 4096)]), (T.odr[:], [("odr", 0, 4096)])) for r in range(16)])
    ts(R("IDf"), R("cc", 0, 8, 1, 8), R("pf", p=8), OP.is_equal)
    ts(R("dW"), R("kk", 0, 192), R("p15"), OP.is_equal)
    ts(R("LT"), R("kk", 0, 192), R("p15"), OP.is_ge, 1000.0, OP.mult)
    ms(R("ZW"), 0.0)
    ms(R("ZZ"), 0.0)
    cp(R("aU"), R("a32"))
    ts(R("aC", 0, 12), R("c16"), R("p15"), OP.add, 4096.0, OP.add)
    ts(R("aC", 12, 24), R("c16"), R("p15"), OP.add, 192.0, OP.add)
    ts(R("pp1"), R("p15"), 1.0, OP.add)

    def thresholds():
        ms(R("oneF"), 1.0)
        cp(R("thf"), R("thi"))
        ts(R("thD"), R("IDf"), R("thf"), OP.mult)
        mm(R("b6", 0, 8, 1, 96), R("oneF"), R("thD"))
        for h in H:
            ts(R("thA", 8 * h, 8 * h + 8), A("b6", 0, 8), 1024.0, OP.mult)

    def late_constants():
        ms(R("X", 4096, 4288), 0.0)
        ms(R("ow", 4096, 4288), 0.0)
        ms(R("oneB"), 1.0)
        cp(R("mb0"), R("mi32"))

    def half(name, h, step=1):
        return R(name, 1536 * h, 1536 * h + 1536, step)

    def gather(v, off, h):
        act(half(v, h), IND("X", 0, 4096, off, 96 * h, 96 * h + 96))

    def begin(bank):
        mm(A(bank, 0, 256), R("one1", 0, 96), R("j64"), True, False)

    def group_sum(bank, src, w, h, stop=False):
        for k in range(16):
            mm(A(bank, 128 * h + k, 128 * h + 128, 16), R(src, 1536 * h + k, 1536 * h + 1536, 16), R(w), False, stop and k == 15)

    def digits(bank, at, i, h, w, start=False, stop=False):
        mm(A(bank, at + 128 * h, at + 128 * h + 128), R("HL", 192 * i + 96 * h, 192 * i + 96 * h + 96), R(w), start, stop)

    def split(m32):
        ts(R("HL32", 0, 192), R(m32), 6, OP.arith_shift_right)
        ts(R("HL32", 192, 384), R(m32), 63, OP.bitwise_and)
        cp(R("HL"), R("HL32"))

    def payload(wide):
        for h in H:
            digits("b2", 0, 1, h, "ID", True, False)
            digits("b2", 0, 0, h, "IDn", False, True)
        act(R("Q1"), A("b2", 0, 256))
        for i in range(2 if wide else 1):
            mm(A("b4", 256 * i, 256 * i + 256), R("one1", 0, 96), R("j128"), True, False)
            for h in H:
                digits("b4", 256 * i, 0, h, "ID" if i else "ID2", False, h == 1 and not i)
                if i:
                    digits("b4", 256 * i, 1, h, "ID", False, h == 1)
        n = 512 if wide else 256
        act(R("Q23", 0, n), A("b4", 0, n))

    def extremes(v, mx, mn, h):
        scan(half(mx, h), R("m01"), half(v, h), OP.mult, OP.max)
        scan(half(mn, h), R("m512"), half(v, h), OP.add, OP.min)

    def centres(mx, mn, s, ci, cz):
        tt(R(s), R(mx, 15, 3072, 16), R(mn, 15, 3072, 16), OP.add)
        ts(R(ci), R(s), 0.5, OP.mult, -0.25, OP.add)
        cp(R(cz, 0, 3072, 16), R(ci))

    def spread(cx, cz, h):
        scan(half(cx, h), R("m01"), half(cz, h), OP.mult, OP.add)

    def larger(v, first, cx, c0, d, h):
        tt(half(v, h, 16), first, half(c0, h, 16), OP.max)
        scan(half(d, h), half(cx, h), half(v, h), OP.min, OP.max)

    def seg(f, lo, hi):
        return A(f, lo + 15, hi, 16)

    def play(t):
        oI, oR, mb = "oI%d" % t, "oR%d" % t, "mb%d" % t
        IC, RC, MR = "IC%d" % t, "RC%d" % t, "MR%d" % t
        last = t == 1
        m96 = R("m01", 0, 256, 1, 96)
        m96x2 = R("m01", 0, 512, 1, 96)
        mB1 = A("mB", 0, 256)
        if t == 0:
            thresholds()
            cp(R("mw"), R(oI))
        gather("VI", oI, 0)
        act(R("VI", 1536, 2304), IND("X", 0, 4096, oI, 96, 144))
        cp(R("VI", 2304, 3072), IND("X", 0, 4096, oI, 144, 192))
        split("mw")
        for h in H:
            extremes("VI", "XI", "NI", h)
        begin("b0")
        for h in H:
            digits("b0", 0, 0, h, "ID")
        payload(False)
        gather("VR", oR, 0)
        for h in H:
            group_sum("b0", "VI", "BN1", h)
        gather("VR", oR, 1)
        centres("XI", "NI", "sI", "CiI", "CZI")
        for h in H:
            spread("CXI", "CZI", h)
            larger("VI", half("VI", h, 16), "CXI", "CZI", "DA", h)
            group_sum("b0", "DA", "BI2", h, h == 1)
        extremes("VR", "XR", "NR", 0)
        u, a0 = A("b3", 0, 256), A("b0", 0, 256)
        scan(R("FI", 0, 256), mB1, a0, OP.add, OP.min)
        tt(R("KI", 0, 256), a0, R("Q1"), OP.add)
        scan(R("FI", 256, 512), mB1, R("KI", 0, 256), OP.add, OP.min)
        cp(R("eI", 0, 32), seg("FI", 0, 512))
        ts(R("e63"), R("eI", 0, 32), 63, OP.bitwise_and)
        tt(R("KI", 512, 768), R("Q23", 0, 256), a0, OP.subtract)
        ts(R("t16"), R("e63", 0, 16), 64.0, OP.mult)
        tt(R("ZS", 0, 256, 16), R("t16"), R("e63", 16, 32), OP.add)
        scan(u, m96, R("ZS"), OP.mult, OP.add)
        tt(R("SXm"), u, R("dA"), OP.mult)
        for h in H:
            mm(R("b7", 6 * h, 6 * h + 6), R("SXm", 128 * h, 128 * h + 128), R("B6"))
        cp(R("sL"), R("b7", 0, 12))
        begin("b5")
        for h in H:
            group_sum("b5", "VR", "BI1", h)
        cp(R("nL"), IND("nbw", 0, 4096, "sL", 0, 12))
        act(R("SW", 0, 12), R("b7", 0, 12))
        for h in H:
            gather("V2", "nL", h)
            act(R("V0", 96 * h, 96 * h + 96), half("V2", h, 16))
        cp(R("bf"), IND("ow", 0, 4096, "sL", 0, 12))
        cp(R("bU"), R("bf"))
        mm(R("b6", 0, 192), R("ID"), R("bf"), True, False)
        mm(R("b6", 0, 192), R("ID"), R("LT"), False, True)
        extremes("VR", "XR", "NR", 1)
        centres("XR", "NR", "sR", "CiR", "CZR")
        cp(R("CRc"), R("CiR"))
        for h in H:
            act(half("CXB", h), IND("CRc", 0, 192, "bU", 96 * h, 96 * h + 96))
        cp(R("n32"), R("nL"))
        split("n32")
        for bank in ("b0", "b1"):
            begin(bank)
            for h in H:
                digits(bank, 0, 0, h, "ID")
        for h in H:
            for bank in ("b0", "b1"):
                group_sum(bank, "V2", "BN1", h)
        scan(R("FI", 512, 768), mB1, R("KI", 512, 768), OP.add, OP.min)
        payload(True)
        act(half("CXR", 1), IND("CRc", 0, 192, "aU", 96, 192))
        cp(R("eI", 32, 48), seg("FI", 512, 768))
        ts(R("kc"), R("eI"), 6, OP.arith_shift_right, 15, OP.bitwise_and)
        cp(R("kfl"), R("kc"))
        tt(R("dk"), R("kfl", 32, 48), R("kfl", 0, 16), OP.subtract)
        if t == 0:
            ms(R("meq", 0, 1936, 176), 0.0)
            ms(R("meq", 1936, 2128, 16), 0.0)
        tt(R("bd"), R("bf"), R("dW"), OP.mult)
        scan(R("bs"), R("m01", 0, 192), R("bd"), OP.mult, OP.add)
        cp(R("SW", 12, 24), R("bs", 15, 192, 16))
        cp(R("ZW", 0, 192, 16), R("bs", 15, 192, 16))
        cp(R("Lb"), R("SW", 12, 24))
        for c in range(1, 12):
            e = 176 * c
            ts(R("EQ", e - 16 * c, e), R("bf", 0, 16 * c), R("SW", 12 + c, 13 + c), OP.is_equal)
        scan(R("bx"), R("m01", 0, 192), R("ZW"), OP.mult, OP.add)
        tt(R("EQ", 1936, 2128), R("b6", 0, 192), R("bx"), OP.is_equal)
        scan(R("EC"), R("meq"), R("EQ"), OP.mult, OP.add)
        cp(R("du"), R("EC", 1951, 2128, 16))
        tt(R("du", 1, 12), R("du", 1, 12), R("EC", 175, 1936, 176), OP.add)
        ts(R("f2", 0, 12), R("du"), 0.0, OP.is_equal)
        ts(R("f2", 12, 24), R("du"), 0.0, OP.is_equal)
        tt(R("l1"), R("SW"), R("aC"), OP.subtract)
        tt(R("l2"), R("l1"), R("f2"), OP.mult)
        tt(R("l3"), R("l2"), R("aC"), OP.add)
        cp(R("LS"), R("l3"))
        for h in H:
            larger("V2", R("V0", 96 * h, 96 * h + 96), "CXI", "CZI", "DA", h)
            group_sum("b0", "DA", "BI2", h, h == 1)
        act(R("ff"), IND("FW", 0, 4288, "LS", 0, 12))
        act(R("fp"), R("ff"), AF.Identity, -1.0, R("pp1"))
        if not last:
            act(R("xg"), IND("X", 0, 4096, "sL", 0, 12), AF.Relu, -16.0)
        for h in H:
            larger("V2", R("V0", 96 * h, 96 * h + 96), "CXB", "CXB", "DB", h)
            group_sum("b1", "DB", "BI2", h, h == 1)
        for i, cz in ((0, "CZI"), (1, "CXB")):
            for h in H:
                mm(A("b7", 16 + 16 * i + 8 * h, 24 + 16 * i + 8 * h), half(cz, h, 16), R("BI1"))
        if t == 0:
            late_constants()
        spread("CXR", "CZR", 0)
        for h in H:
            larger("VR", half("VR", h, 16), "CXR", "CZR", "DA", h)
            group_sum("b5", "DA", "BN2", h, h == 1)
        ui, ur = a0, A("b1", 0, 256)
        q1, q2, q3 = R("Q1"), R("Q23", 0, 256), R("Q23", 256, 512)
        scan(R("FI", 0, 256), mB1, ui, OP.add, OP.min)
        tt(R("KI", 256, 512), q2, ui, OP.subtract)
        tt(R("KI", 512, 768), ui, q1, OP.add)
        tt(R("KI", 768, 1024), q3, ui, OP.subtract)
        scan(R("FI", 256, 1024), A("mB", 256, 1024), R("KI", 256, 1024), OP.add, OP.min)
        if not last:
            cp_scatter(IND("X", 0, 4288, "LS", 0, 12), R("xg"))
        for i in (0, 1):
            tt(R("ZL", 256 * i, 256 * i + 256, 16), A("b7", 16 + 16 * i, 32 + 16 * i), R("thA"), OP.add)
        scan(R("LX"), m96x2, R("ZL"), OP.mult, OP.add)
        tt(R("FM", 0, 256), ui, R("LX", 0, 256), OP.is_lt)
        tt(R("FM", 256, 512), ur, R("LX", 256, 512), OP.is_lt)
        scan(R("CN"), m96x2, R("FM"), OP.mult, OP.add)
        tt(R("w4", 0, 16), seg("CN", 0, 256), seg("CN", 256, 512), OP.is_gt)
        for i in (1, 2, 3):
            act(R("w4", 16 * i, 16 * i + 16), R("w4", 0, 16))
        act(R("ZK", 256, 512, 16), R("w4", 0, 16))
        tt(R("dw"), R("dk"), R("w4", 0, 16), OP.mult)
        tt(R("ZK", 0, 256, 16), R("dw"), R("kfl", 0, 16), OP.add)
        tt(R("KR", 0, 256), q2, ur, OP.subtract)
        scan(R("FR", 256, 512), mB1, ur, OP.add, OP.min)
        scan(R("KX"), m96x2, R("ZK"), OP.mult, OP.add)
        tt(R("KR", 256, 512), q3, ur, OP.subtract)
        tt(R("KR", 512, 768), ur, q1, OP.add)
        scan(R("FR", 0, 256), mB1, R("KR", 0, 256), OP.add, OP.min)
        scan(R("FR", 512, 1024), A("mB", 0, 512), R("KR", 256, 768), OP.add, OP.min)
        scan(R("FD"), mB1, A("b5", 0, 256), OP.add, OP.min)
        cp(R("eD"), seg("FD", 0, 256))
        ts(R("fD"), R("eD"), 6, OP.arith_shift_right, 15, OP.bitwise_and)
        cp(R("ZR", 0, 256, 16), R("fD"))
        scan(R("RX"), m96, R("ZR"), OP.mult, OP.add)
        for h in H:
            mm(R("b6", 96 * h, 96 * h + 96), R("RX", 128 * h, 128 * h + 128), R("ID", 0, 96, 1, 96))
        ts(R("mR"), R("b6", 0, 192), R("p15"), OP.is_equal)
        act(R("mRa"), IND("mR", 0, 192, "Lb", 0, 12))
        for i in range(4):
            mm(R("b6", 96 * i, 96 * i + 96), R("KX", 128 * i, 128 * i + 128), R("ID", 0, 96, 1, 96))
        tt(R("s1"), seg("FI", 0, 1024), seg("FR", 0, 1024), OP.subtract)
        tt(R("s2"), R("s1"), R("w4"), OP.mult)
        tt(R("s3"), R("s2"), seg("FR", 0, 1024), OP.add)
        ts(R("s4"), R("s3"), 63, OP.bitwise_and)
        ts(R("ZZ", 0, 512, 16), R("s4", 0, 32), 128.0, OP.add)
        cp(R("ZZ", 512, 1024, 16), R("s4", 32, 64))
        for i, bank in ((0, "b5"), (1, "b4")) if last else ((1, "b4"), (0, "b5")):
            for d in (0, 512):
                scan(R("ZX", d + 256 * i, d + 256 * i + 256), m96, R("ZZ", d + 256 * i, d + 256 * i + 256), OP.mult, OP.add)
            for h in H:
                for d, w in ((0, "ID64"), (512, "ID")):
                    mm(R(bank, 96 * h, 96 * h + 96), R("ZX", d + 256 * i + 128 * h, d + 256 * i + 128 * h + 128), R(w, 0, 96, 1, 96), d == 0, d > 0)
        tt(R("ox"), R("bf"), R("b6", 192, 384), OP.add)
        ts(R("oy"), R("ox"), 192.0, OP.is_lt)
        tt(R("ov"), R("ox"), R("oy"), OP.mult)
        act(R("zr"), R("b4", 0, 192), AF.Identity, -4096.0)
        tt(R("mk"), R("b6", 0, 192), R("fp"), OP.is_equal)
        tt(R(IC), R("b5", 0, 192), R("mk"), OP.mult)
        if not last:
            send(IC, [(dn1, "inA", "rA"), (up1, "inB", "rB")])
        else:
            send(IC, [(dn2, "inC", "rC")])
        tt_scatter(IND(RC, 0, 384, "LS", 12, 24), R("zr"), R("mRa"), OP.mult)
        tt(R(MR), R(RC, 0, 192), R(mb), OP.max)
        if not last:
            send(MR, [(up2, "inM", "rR")])
        cp_scatter(IND("ow", 0, 4288, "LS", 0, 12), R("ov"))
        if last:
            dma("g", [((T.yown[:], []), (T.ow[0:128:16, 0:4096], [("ow", 0, 4096)]))])
            return
        tt(R("wf"), R("b6", 192, 384), R("ff"), OP.mult)
        act(R("wg"), R("wf"), acc=R("wc"))
        act(R("wb"), R("wc"))
        mm(A("b7", 48, 49), R("oneB"), R("wb"))
        ts(R("wi"), A("b7", 48, 49), 0.0625, OP.mult)
        ts(R("wj"), R("wi"), 63, OP.bitwise_and)
        ts(R("wk"), R("wj"), 1024.0, OP.mult)

    def merged(old, new, words):
        tt(R("mv"), R(old), R(new), OP.max)
        ts(R(words), R("mv"), 4095, OP.bitwise_and)

    play(0)
    landed("inA", "rA", n16 // 2)
    landed("inB", "rB", n16 // 2)
    landed("inM", "rR", n16)
    merged("MR0", "inA", "mi32")
    cp(R("oR1"), R("mi32"))
    merged("inM", "inB", "mw")
    cp(R("oI1"), R("mw"))
    cp(R("mb1"), R("mi32"))
    ts(R("thA"), R("thA"), R("wk"), OP.add)
    play(1)
    landed("inC", "rC", n16)
    merged("MR1", "inC", "mi32")
    cp(R("yo"), R("mi32"))
    dma("s", [((T.ym[:], []), R("yo"))])
    for q in ("v", "a", "p", "g"):
        g.wait_ge(S["q" + q], count[q])
    for sem, val in loc_done:
        g.wait_ge(S[sem], val)
    g.wait_ge(S["d%d" % (ndma[0] - 2)], 16)
    g.sync.wait_ge(S["d%d" % (ndma[0] - 1)], 16)
